import numpy as np, ml_dtypes
CORES = [23,119,17,113]
N = 4
import mx_ref
BF = ml_dtypes.bfloat16
def cols(t, e):
    v = np.concatenate([t.reshape(128, -1, 4), np.zeros((128, 1, 4), BF)], axis=1)
    return np.ascontiguousarray(v[:, e]).reshape(128, -1)
def decode(q):
    o = []
    for b in range(4):
        e = np.zeros((128, 128, 4), np.float32); e[np.arange(128), np.arange(128), b] = 1
        o.append(mx_ref.matmul(mx_ref.quantize(e.reshape(128, 512).astype(BF)), q))
    return np.stack(o, axis=2).reshape(128, -1)
def f(rng, *shape):
    return mx_ref.flush((rng.standard_normal(shape, dtype=np.float32) * np.exp2(rng.integers(-2, 3, shape[:-1] + (1,)))).astype(BF))
def wide(rng, *shape, cols=0):
    v = rng.standard_normal(shape, dtype=np.float32) * np.exp2(rng.integers(-12, 13, shape)).astype(np.float32)
    if cols: v *= np.repeat(np.exp2(rng.integers(-cols, cols + 1, shape[:-2] + (1, shape[-1] // 4))) * (rng.random(shape[:-2] + (1, shape[-1] // 4)) > 0.0625), 4, axis=-1).astype(np.float32)
    return mx_ref.flush(v.astype(BF))
T, K = 512, 128
def setup_inputs(rng):
    u = np.zeros((N, 128, 512), BF); u[:, :, :4] = f(rng, N, 128, 4)
    return {"gr": f(rng, N, 128, 4 * T), "u": u}
def raised(rng, chosen):
    d = setup_inputs(rng)
    for r in range(N):
        g = d["gr"][r].astype(np.float32).reshape(128, T, 4)
        sign = np.where(d["u"][r][:, :4].astype(np.float32) < 0, -1, 1).reshape(128, 1, 4) * rng.choice([-1, 1], K).reshape(1, K, 1)
        v = g * np.float32(2.0 ** -8)
        v[:, chosen[r]] = np.abs(g[:, chosen[r]]) * sign
        d["gr"][r] = mx_ref.flush(v.reshape(128, 4 * T).astype(BF))
    return d
def setup_inputs_same(rng):
    d = raised(rng, [rng.permutation(T)[:K]] * N)
    k = rng.permutation(np.concatenate([[12, -12, -11], rng.integers(-12, 13, N - 3)]))
    d["gr"] = mx_ref.flush((d["gr"].astype(np.float32) * np.exp2(k).astype(np.float32).reshape(N, 1, 1)).astype(BF))
    return d
def setup_inputs_apart(rng):
    p = rng.permutation(T)
    return raised(rng, [p[(r * K + np.arange(K)) % T] for r in range(N)])
def setup_inputs_ties(rng):
    d = setup_inputs(rng); n = T // 11
    for r in range(N):
        p = rng.permutation(T)[:11 * n]
        e = np.full(T, -1); e[p] = np.repeat(np.arange(n), 11)
        s = rng.choice([-1, 1], (n, 11)); s[:, 0] = 1; s[:, 1] = -1
        sign = np.ones(T, np.float32); sign[p] = s.reshape(-1)
        d["gr"][r] = (cols(d["gr"][r], e).astype(np.float32).reshape(128, T, 4) * sign.reshape(1, T, 1)).reshape(128, 4 * T).astype(BF)
    return d
def setup_inputs_few(rng):
    d = setup_inputs(rng); p = rng.permutation(N)
    d["u"][p[0]] = 0
    sign = rng.choice([-1, 1], (128, 1, 4))
    d["u"][p[1]][:, :4] = (sign * rng.uniform(1, 4, (128, 1, 4)) * 2.0 ** 28).reshape(128, 4).astype(BF)
    d["gr"][p[1]] = (sign * rng.choice([-1, 1], (1, T, 1)) * rng.uniform(1, 4, (128, T, 4)) * 2.0 ** 28).reshape(128, 4 * T).astype(BF)
    for r in p[2:2 + N // 2]:
        k = rng.permutation(T)[:rng.integers(1, K)]
        e = np.full(T, -1); e[k] = k
        d["gr"][r] = cols(d["gr"][r], e)
    return d
def setup_inputs_spread(rng):
    d = setup_inputs(rng); d["gr"] = wide(rng, N, 128, 4 * T, cols=8); return d
def check_inputs(d):
    return ["u"] if (d["u"][:, :, 4:].astype(np.float32) != 0).any() else []
def reference(gr, u):
    acc = np.zeros((128, T, 4), np.float32); nb = np.zeros((N, K), np.float32); sc = np.zeros((N, 1, K), np.float32)
    er = gr.astype(np.float32).reshape(N, 128, T, 4)
    for s in range(N):
        score = np.abs(mx_ref.matmul(mx_ref.quantize(u[s]), mx_ref.quantize(gr[s]))[0]) + np.float32(0.0)
        e = np.argsort(-score, kind="stable")[:K]
        v = decode(mx_ref.quantize(cols(gr[s], e))).reshape(128, K, 4)
        acc[:, e] = acc[:, e] + v
        er[s][:, e] = er[s][:, e] - v
        nb[s] = e
        sc[s, 0] = score[e]
    return {"acc": np.stack([acc.reshape(128, 4 * T)] * N), "er": er.reshape(N, 128, 4 * T), "nb": np.stack([nb] * N), "sc": sc}

@@ -1,0 +1,378 @@
+from concourse.bass import DstId, RemoteDMATransfer
+from concourse.mybir import dt, AluOpType as A, ActivationFunctionType as F
+
+NR = 4
+K = 128
+ZB = 16
+TW = ZB + 512 * NR
+X4, U8, F32, BF, I32, U16 = "float8_e4m3fn_x4", "uint8", "float32", "bfloat16", "int32", "uint16"
+
+SCRATCH = {
+    "u4": ("sbuf", [128, 16], BF), "grt": ("sbuf", [128, 2048], BF), "urep": ("sbuf", [128, 512], BF),
+    "sel": ("sbuf", [128, 512], BF), "ones": ("sbuf", [128, 520], BF), "ew": ("sbuf", [128, 520], BF),
+    "uq": ("sbuf", [128, 128], X4), "us": ("sbuf", [128, 128], U8),
+    "gq": ("sbuf", [128, 512], X4), "gs": ("sbuf", [128, 512], U8),
+    "eq": ("sbuf", [128, 512], X4), "es": ("sbuf", [128, 512], U8),
+    "psa": ("psum", [128, 2048], F32), "psb": ("psum", [128, 2048], F32),
+    "pi": ("sbuf", [128, 32], I32), "t3": ("sbuf", [128, 32], I32), "uof": ("sbuf", [128, 32], U16),
+    "p4i": ("sbuf", [128, 8], I32), "p16i": ("sbuf", [128, 8], I32),
+    "tcol": ("sbuf", [128, 8], F32), "p4f": ("sbuf", [128, 8], F32), "p16f": ("sbuf", [128, 8], F32),
+    "tz": ("sbuf", [128, 8], F32),
+    "ji": ("sbuf", [128, 512], I32), "m4": ("sbuf", [128, 512], I32), "jf": ("sbuf", [128, 512], F32),
+    "mk4": ("sbuf", [128, 512], F32), "rst": ("sbuf", [128, 512], F32),
+    "gi": ("sbuf", [128, 64], F32), "gd": ("sbuf", [128, 64], F32),
+    "sab": ("sbuf", [128, 512], F32), "scol": ("sbuf", [128, 4], F32), "k1": ("sbuf", [128, 512], F32),
+    "cmp": ("sbuf", [128, 2560], BF), "junk": ("sbuf", [128, 2560], BF), "cnt": ("sbuf", [128, 4], F32),
+    "scn": ("sbuf", [128, 128], BF), "rof": ("sbuf", [128, 4], U16),
+    "win": ("sbuf", [128, 512], F32), "win2": ("sbuf", [128, 8, 32], F32), "tr": ("sbuf", [128, 8, 32], F32),
+    "a0": ("sbuf", [128, 8], F32), "a1": ("sbuf", [128, 8], F32), "a2": ("sbuf", [128, 8], F32),
+    "ofs": ("sbuf", [128, 32], U16),
+    "er32": ("sbuf", [128, 2048], F32), "dif": ("sbuf", [128, 512], F32),
+    "tab": ("sbuf", [128, TW], F32), "pw": ("sbuf", [128, 512], F32), "dat": ("sbuf", [128, 512], F32),
+    "pv": ("sbuf", [128, 384], F32), "pvs": ("sbuf", [128, 384], F32), "pof": ("sbuf", [128, 96], U16),
+    "lw": ("sbuf", [128, 512], F32), "lws": ("sbuf", [128, 512], F32), "lof": ("sbuf", [128, 128], U16),
+    "gsum": ("sbuf", [128, 512], F32), "accs": ("sbuf", [128, 2048], F32),
+    "nbl": ("sbuf", [128, 512], F32), "scb": ("sbuf", [128, 128], F32),
+}
+for _s in range(NR):
+    SCRATCH["lst%d" % _s] = ("sbuf", [128, 8], U16)
+    SCRATCH["q%d" % _s] = ("sbuf", [128, 128], X4)
+    SCRATCH["p%d" % _s] = ("sbuf", [128, 128], U8)
+
+SEMAPHORES = (["gp", "ve", "se", "te", "left", "ldu", "ster", "stnb", "stsc"]
+              + ["ld%d" % i for i in range(4)] + ["sta%d" % i for i in range(4)]
+              + ["al%d" % i for i in range(NR)] + ["ac%d" % i for i in range(NR)])
+
+
+def engines_of(src, cores, topo):
+    dsts = [c for c in cores if c != src]
+    off = [c for c in dsts if topo.chip(c) != topo.chip(src)]
+    on = [c for c in dsts if c not in off]
+    plan, used = {}, []
+    for i, c in enumerate(off):
+        e = topo.engines(src, c)
+        n = len(e) // len(off)
+        plan[c] = e[i * n:(i + 1) * n]
+        used += plan[c]
+    for i, c in enumerate(on):
+        e = [x for x in topo.engines(src, c) if x not in used]
+        n = len(e) // len(on)
+        plan[c] = e[i * n:(i + 1) * n]
+    return plan
+
+
+def rank_program(g, core, T, topo):
+    rank = T.rank_of(core)
+    if rank is None:
+        return
+    queues = {"g": g, "v": g.vector, "s": g.scalar, "t": g.tensor, "y": g.sync}
+    count = {"gp": 0, "ve": 0, "se": 0, "te": 0}
+    own = {"g": "gp", "v": "ve", "s": "se", "t": "te"}
+    seen = {}
+
+    def need(q, *toks):
+        best = {}
+        for tk in toks:
+            best[tk[0]] = max(best.get(tk[0], 0), tk[1])
+        for sem in best:
+            if seen.get((q, sem), 0) < best[sem]:
+                queues[q].wait_ge(T.sem[sem], best[sem])
+                seen[(q, sem)] = best[sem]
+
+    def did(q, ins):
+        sem = own[q]
+        ins.then_inc(T.sem[sem], 1)
+        count[sem] += 1
+        return (sem, count[sem])
+
+    def dma(q, sem, out, in_):
+        queues[q].dma_start(out, in_).then_inc(T.sem[sem], 16)
+        return (sem, 16)
+
+    V, S, TE, Y = g.vector, g.scalar, g.tensor, g.sync
+    me = rank
+    mates = [s for s in range(NR) if s != me and topo.chip(T.cores[s]) == topo.chip(core)]
+    late = [s for s in range(NR) if s != me and s not in mates]
+    plan = engines_of(core, T.cores, topo)
+    narr = {s: len(engines_of(T.cores[s], T.cores, topo)[core]) for s in range(NR) if s != me}
+
+    ldu = dma("y", "ldu", T.u4[:, 0:4], T.u[:, 0:4])
+    ld = {}
+    for a in range(4):
+        ld[a] = dma("s" if a % 2 == 0 else "y", "ld%d" % a, T.grt[:, 512 * a:512 * a + 512], T.gr[:, 512 * a:512 * a + 512])
+
+    k_ones = did("v", V.memset(T.ones[:, :], 1.0))
+    k_win = did("v", V.memset(T.win[:, 0:128], 0.0))
+    k_tab = did("v", V.memset(T.tab[:, 0:ZB], 0.0))
+    k_pi = did("g", g.iota(T.pi[:, :], [[0, 32]], 0, 1))
+    k_ji = did("g", g.iota(T.ji[:, :], [[1, 512]], 0, 0))
+    k_gi = did("g", g.iota(T.gi[:, :], [[128, 4], [1, 16]], 0, 0, allow_small_or_imprecise_dtypes=True))
+    need("g", k_ones)
+    k_ew = did("g", g.affine_select(T.ew[:, :], T.ones[:, :], [[1, 520]], A.is_equal, 0.0, -4, -4))
+    k_jf = did("g", g.iota(T.jf[:, :], [[1, 512]], 0, 0, allow_small_or_imprecise_dtypes=True))
+
+    need("v", k_pi)
+    c1 = did("v", V.tensor_scalar(T.t3[:, :], T.pi[:, :], 3, None, A.bitwise_and))
+    c2 = did("v", V.tensor_scalar(T.p4i[:, 0:1], T.pi[:, 0:1], 2, 3, A.arith_shift_right, A.bitwise_and))
+    c3 = did("v", V.tensor_scalar(T.p16i[:, 0:1], T.pi[:, 0:1], 112, None, A.bitwise_and))
+    need("v", c1)
+    k_uof = did("v", V.tensor_copy(T.uof[:, :], T.t3[:, :]))
+    k_tcol = did("v", V.tensor_copy(T.tcol[:, 0:1], T.t3[:, 0:1]))
+    need("v", c3)
+    k_p4 = did("v", V.tensor_copy(T.p4f[:, 0:1], T.p4i[:, 0:1]))
+    k_p16 = did("v", V.tensor_copy(T.p16f[:, 0:1], T.p16i[:, 0:1]))
+    need("v", k_tcol)
+    k_tz = did("v", V.tensor_scalar(T.tz[:, 0:1], T.tcol[:, 0:1], float(ZB), None, A.add))
+    need("v", k_ji)
+    k_m4 = did("v", V.tensor_scalar(T.m4[:, :], T.ji[:, :], 3, None, A.bitwise_and))
+    need("v", k_m4, k_p4)
+    k_mk4 = did("v", V.tensor_scalar(T.mk4[:, :], T.m4[:, :], T.p4f[:, 0:1], None, A.is_equal))
+    need("v", k_uof, ldu)
+    k_ur = did("v", V.tensor_copy(T.urep[:, :], T.u4[:, 0:4].indirect(T.uof[:, :])))
+    need("v", k_ur)
+    k_uq = did("v", V.quantize_mx(T.uq[:, :], T.us[:, :], T.urep[:, :]))
+    k_rst = did("v", V.tensor_scalar(T.rst[:, :], T.m4[:, :], 0.0, None, A.not_equal))
+    need("v", k_gi, k_p16)
+    k_gd = did("v", V.tensor_scalar(T.gd[:, :], T.gi[:, :], T.p16f[:, 0:1], None, A.add))
+
+    need("s", k_jf, k_tz)
+    k_dat = did("s", S.activation(T.dat[:, :], T.jf[:, :], F.Identity, bias=T.tz[:, 0:1], scale=4.0))
+    k_pw = did("s", S.activation(T.pw[:, :], T.jf[:, :], F.Identity, bias=T.tcol[:, 0:1], scale=0.0))
+
+    k_gq, k_row, k_col, k_abs = {}, {}, {}, {}
+    for a in range(4):
+        need("v", ld[a])
+        c = slice(128 * a, 128 * a + 128)
+        k_gq[a] = did("v", V.quantize_mx(T.gq[:, c], T.gs[:, c], T.grt[:, 512 * a:512 * a + 512]))
+        need("t", k_uq, k_gq[a])
+        o = slice(512 * a, 512 * a + 128)
+        k_row[a] = did("t", TE.matmul_mx(T.psa[:, o], T.uq[:, :], T.us[:, :], T.gq[:, c], T.gs[:, c], True, True))
+        k_col[a] = did("t", TE.matmul_mx(T.psb[:, o], T.gq[:, c], T.gs[:, c], T.uq[:, :], T.us[:, :], True, True))
+        need("s", k_row[a])
+        k_abs[a] = did("s", S.activation(T.sab[:, c], T.psa[:, o], F.Abs))
+    need("s", k_col[3])
+    k_scol = did("s", S.activation(T.scol[:, 0:4], T.psb[:, 0:1537:512], F.Abs))
+    need("g", k_abs[3])
+    k_k1 = did("g", g.affine_select(T.k1[:, :], T.sab[:, :], [[0, 4], [-1, 128]], A.is_gt, -1.0, 0, 1))
+    k_eq = {}
+    need("v", k_ew)
+    for b in range(4):
+        c = slice(128 * b, 128 * b + 128)
+        k_eq[b] = did("v", V.quantize_mx(T.eq[:, c], T.es[:, c], T.ew[:, 4 - b:516 - b]))
+
+    k_cmp = {}
+
+    def main(a):
+        sc, o, n = T.scol[:, a:a + 1], 640 * a, 128 * a
+        if n:
+            k_cmp[a, 0] = did("v", V.tensor_scalar(T.cmp[:, o:o + n], T.sab[:, 0:n], sc, None, A.is_ge))
+        k_cmp[a, 1] = did("v", V.tensor_scalar(T.cmp[:, o + n:o + 512], T.sab[:, n:512], sc, None, A.is_gt))
+
+    def ties(a):
+        need("v", k_k1)
+        k_cmp[a, 2] = did("v", V.tensor_scalar(T.cmp[:, 640 * a + 512:640 * a + 640], T.k1[:, 128 * a:128 * a + 128],
+                                               T.scol[:, a:a + 1], None, A.is_equal))
+
+    need("v", k_scol, k_abs[3])
+    main(0)
+    main(1)
+    ties(0)
+    ties(1)
+    main(2)
+    ties(2)
+    main(3)
+    ties(3)
+    k_cnt = {}
+    for a in range(3):
+        need("s", k_cmp[a, 2])
+        o = slice(640 * a, 640 * a + 640)
+        k_cnt[a] = did("s", S.activation(T.junk[:, o], T.cmp[:, o], F.Copy, accum_out=T.cnt[:, a:a + 1]))
+    need("s", k_cmp[3, 0])
+    k_cnt[3] = did("s", S.activation(T.junk[:, 1920:2304], T.cmp[:, 1920:2304], F.Copy, accum_out=T.cnt[:, 3:4]))
+    need("v", k_cmp[3, 2])
+    k_scn = did("v", V.tensor_tensor_scan(T.scn[:, :], T.cmp[:, 2304:2432], T.cmp[:, 2432:2560], 0.0, A.add, A.add))
+    need("v", k_cnt[2])
+    k_r0 = did("v", V.tensor_copy(T.rof[:, 0:3], T.cnt[:, 0:3]))
+    need("v", k_cnt[3], k_scn)
+    k_r1 = did("v", V.tensor_scalar(T.rof[:, 3:4], T.scn[:, 127:128], T.cnt[:, 3:4], None, A.add))
+
+    need("v", k_r1, k_win, k_gd)
+    k_w = did("v", V.tensor_copy(T.win[:, 0:512].indirect(T.rof[:, 0:4]), T.gd[:, :]))
+    need("v", k_w)
+    need("s", k_w)
+    d1 = did("v", V.tensor_copy(T.win2[:, :, 0:16], T.win[:, 0:128]))
+    d2 = did("s", S.activation(T.win2[:, :, 16:32], T.win[:, 0:128], F.Copy))
+    need("v", d1, d2)
+    k_tr = did("v", V.transpose(T.tr[:, :, :], T.win2[:, :, :]))
+    need("v", k_tr)
+    k_a0 = did("v", V.tensor_tensor(T.a0[:, :], T.tr[:, :, 0], T.tr[:, :, 16], A.add))
+    need("v", k_a0)
+    for h in range(2):
+        k_a1 = did("v", V.tensor_tensor(T.a1[64 * h:64 * h + 64, :], T.a0[0:64, :], T.a0[64:128, :], A.add))
+    need("v", k_a1)
+    for b in range(4):
+        h = 64 * (b // 2)
+        k_a2 = did("v", V.tensor_tensor(T.a2[32 * b:32 * b + 32, :], T.a1[h:h + 32, :], T.a1[h + 32:h + 64, :], A.add))
+    lists = [T["lst%d" % s] for s in range(NR)]
+    qs = [T["q%d" % s] for s in range(NR)]
+    ps = [T["p%d" % s] for s in range(NR)]
+    need("v", k_a2)
+    k_lst = did("v", V.tensor_copy(lists[me][:, :], T.a2[:, :]))
+    k_of = {}
+    for t in (2, 3, 0, 1):
+        k_of[t] = did("v", V.tensor_scalar(T.ofs[:, 8 * t:8 * t + 8], T.a2[:, :], 4.0, float(t), A.mult, A.add))
+    k_sel = {}
+    for t in (0, 1):
+        need("v", k_of[t])
+        k_sel[t] = did("v", V.tensor_copy(T.sel[:, t:512:4], T.grt[:, 0:2048].indirect(T.ofs[:, 8 * t:8 * t + 8])))
+
+    k_er = {}
+
+    def widen(a):
+        o = slice(512 * a, 512 * a + 512)
+        need("s", ld[a])
+        k_er[a] = did("s", S.activation(T.er32[:, o], T.grt[:, o], F.Copy))
+
+    widen(0)
+    widen(1)
+    for t in (2, 3):
+        need("s", k_of[t])
+        k_sel[t] = did("s", S.activation(T.sel[:, t:512:4], T.grt[:, 0:2048].indirect(T.ofs[:, 8 * t:8 * t + 8]), F.Copy))
+    widen(2)
+    widen(3)
+    need("v", k_sel[1], k_sel[3])
+    k_q = did("v", V.quantize_mx(qs[me][:, :], ps[me][:, :], T.sel[:, :]))
+
+    sent = [0]
+
+    def send(src, dst, sem):
+        tr = []
+        for c in plan:
+            rid, pid, _ = topo.addr(c)
+            tr.append(RemoteDMATransfer(dst_ids=[DstId(rid=rid, pnc=pid)], dma_engine_mask=sum(1 << e for e in plan[c]),
+                                        remote_sem=T.sem[sem], src=src, dst=dst))
+            sent[0] += len(plan[c])
+        g.remote_dma_fused(tr, local_sem=T.sem.left)
+
+    need("g", k_lst)
+    send(lists[me][:, :], lists[me][:, :], "al%d" % me)
+    need("g", k_q)
+    send(qs[me][:, :].bitcast(dt.uint8), qs[me][:, :].bitcast(dt.uint8), "ac%d" % me)
+    send(ps[me][:, :], ps[me][:, :], "ac%d" % me)
+
+    def decode(s, bank, *toks):
+        need("t", k_eq[3], *toks)
+        r = {}
+        for b in range(4):
+            r[b] = did("t", TE.matmul_mx(bank[:, 512 * b:512 * b + 128], T.eq[:, 128 * b:128 * b + 128],
+                                         T.es[:, 128 * b:128 * b + 128], qs[s][:, :], ps[s][:, :], True, True))
+        return r
+
+    def column(s, b):
+        return T.tab[:, ZB + 512 * s + b:ZB + 512 * s + 512:4]
+
+    got = {s: ("ac%d" % s, 2 * narr[s]) for s in narr}
+    heard = {s: ("al%d" % s, narr[s]) for s in narr}
+    heard[me] = k_lst
+    k_v = {}
+    dec = decode(me, T.psa, k_q, k_abs[3])
+    need("t", k_scol)
+    k_sc = did("t", TE.matmul_mx(T.psb[:, 0:128], T.uq[:, :], T.us[:, :], qs[me][:, :], ps[me][:, :], True, True))
+    k_dif = {}
+    for b in range(4):
+        need("v", dec[b])
+        k_dif[b] = did("v", V.tensor_tensor(T.dif[:, 128 * b:128 * b + 128], T.sel[:, b:512:4],
+                                            T.psa[:, 512 * b:512 * b + 128], A.subtract))
+    need("v", k_er[3], *k_dif.values())
+    k_ers = did("v", V.tensor_copy(T.er32[:, 0:2048].indirect(T.ofs[:, 0:32]), T.dif[:, :]))
+    need("y", k_ers)
+    ends = [dma("y", "ster", T.er[:, :], T.er32[:, :])]
+    k_v[me] = []
+    for b in range(4):
+        need("s", k_dif[b])
+        k_v[me].append(did("s", S.activation(column(me, b), T.psa[:, 512 * b:512 * b + 128], F.Copy)))
+    need("s", k_sc)
+    k_scb = did("s", S.activation(T.scb[:, :], T.psb[:, 0:128], F.Abs))
+    need("y", k_scb)
+    ends.append(dma("y", "stsc", T.sc[:, :], T.scb[0:1, :]))
+
+    need("v", k_dat, k_pw, k_mk4)
+    k_pv = k_sca = None
+    for s in range(NR):
+        need("v", heard[s])
+        if s:
+            need("v", k_sca)
+            k_pv = did("v", V.tensor_tensor(T.pv[:, 128 * s - 128:128 * s], T.pw[:, 0:512].indirect(lists[s][:, 0:8]),
+                                            T.mk4[:, 0:128], A.mult))
+            need("v", k_pv)
+        k_sca = did("v", V.tensor_copy(T.pw[:, 0:512].indirect(lists[s][:, 0:8]), T.dat[:, 128 * s:128 * s + 128]))
+    need("v", k_pv, k_rst)
+    k1 = did("v", V.tensor_tensor_scan(T.pvs[:, :], T.rst[:, 0:384], T.pv[:, :], 0.0, A.mult, A.add))
+    need("v", k_sca)
+    k2 = did("v", V.tensor_tensor(T.lw[:, :], T.pw[:, :], T.mk4[:, :], A.mult))
+    need("v", k1)
+    k_pof = did("v", V.tensor_copy(T.pof[:, :], T.pvs[:, 3:384:4]))
+    need("v", k2)
+    k3 = did("v", V.tensor_tensor_scan(T.lws[:, :], T.rst[:, :], T.lw[:, :], 0.0, A.mult, A.add))
+    need("v", k3)
+    k_lof = did("v", V.tensor_copy(T.lof[:, :], T.lws[:, 3:512:4]))
+
+    prev = [k_scb]
+    for s in mates:
+        dec = decode(s, T.psb, got[s], *prev)
+        k_v[s] = []
+        for b in range(4):
+            need("s", dec[b])
+            k_v[s].append(did("s", S.activation(column(s, b), T.psb[:, 512 * b:512 * b + 128], F.Copy)))
+        prev = k_v[s]
+    k_nb = None
+    for s in range(NR):
+        need("s", heard[s])
+        k_nb = did("s", S.activation(T.nbl[:, 128 * s:128 * s + 128], T.jf[:, 0:512].indirect(lists[s][:, 0:8]), F.Copy))
+    need("y", k_nb)
+    ends.append(dma("y", "stnb", T.nb[:, :], T.nbl[0:1, :]))
+
+    x, y = late
+    dx = decode(x, T.psa, got[x], *k_v[me])
+    dy = decode(y, T.psb, got[y], *prev)
+    need("v", k_tab)
+    if x == 0:
+        k_v[x] = []
+        for b in (2, 3):
+            need("s", dx[b])
+            k_v[x].append(did("s", S.activation(column(x, b), T.psa[:, 512 * b:512 * b + 128], F.Copy)))
+        for b in (0, 1):
+            need("v", dx[b])
+            k_v[x].append(did("v", V.tensor_copy(column(x, b), T.psa[:, 512 * b:512 * b + 128])))
+    k_v[y] = []
+    for b in range(4):
+        need("s", dy[b])
+        k_v[y].append(did("s", S.activation(column(y, b), T.psb[:, 512 * b:512 * b + 128], F.Copy)))
+    total = list(k_v[0]) if 0 in k_v else []
+    for s in range(1, NR):
+        need("v", k_pof, k_tab, *total)
+        window = T.tab[:, 0:ZB + 512 * s].indirect(T.pof[:, 32 * s - 32:32 * s])
+        if s == x:
+            k_gs = did("v", V.tensor_copy(T.gsum[:, :], window))
+            need("v", k_gs)
+            for b in range(4):
+                need("v", dx[b])
+                total.append(did("v", V.tensor_tensor(column(s, b), T.gsum[:, b:512:4], T.psa[:, 512 * b:512 * b + 128], A.add)))
+        else:
+            need("v", *k_v[s])
+            o = T.tab[:, ZB + 512 * s:ZB + 512 * s + 512]
+            total.append(did("v", V.tensor_tensor(o, window, o, A.add)))
+    need("v", k_lof, *total)
+    need("s", k_lof, k_tab, *total)
+    for i in range(4):
+        o = T.accs[:, 512 * i:512 * i + 512]
+        window = T.tab[:, 0:TW].indirect(T.lof[:, 32 * i:32 * i + 32])
+        if i % 2 == 0:
+            k = did("v", V.tensor_copy(o, window))
+        else:
+            k = did("s", S.activation(o, window, F.Copy))
+        need("y", k)
+        ends.append(dma("y", "sta%d" % i, T.acc[:, 512 * i:512 * i + 512], o))
+
+    need("y", *ends)
+    need("g", ("left", sent[0]), *[(sem, count[sem]) for sem in ("gp", "ve", "se", "te")])

@@ -16,14 +16,15 @@ SCRATCH = {
     "psa": ("psum", [128, 2048], F32), "psb": ("psum", [128, 2048], F32),
     "pi": ("sbuf", [128, 32], I32), "t3": ("sbuf", [128, 32], I32), "uof": ("sbuf", [128, 32], U16),
     "p4i": ("sbuf", [128, 8], I32), "p16i": ("sbuf", [128, 8], I32),
-    "tcol": ("sbuf", [128, 8], F32), "p4f": ("sbuf", [128, 8], F32), "p16f": ("sbuf", [128, 8], F32),
+    "tcol": ("sbuf", [128, 8], F32), "p4n": ("sbuf", [128, 8], F32), "p16f": ("sbuf", [128, 8], F32),
     "tz": ("sbuf", [128, 8], F32),
-    "ji": ("sbuf", [128, 512], I32), "m4": ("sbuf", [128, 512], I32), "jf": ("sbuf", [128, 512], F32),
+    "m4": ("sbuf", [128, 512], F32), "m4d": ("sbuf", [128, 512], F32), "jf": ("sbuf", [128, 512], F32),
     "mk4": ("sbuf", [128, 512], F32), "rst": ("sbuf", [128, 512], F32),
     "gi": ("sbuf", [128, 64], F32), "gd": ("sbuf", [128, 64], F32),
     "sab": ("sbuf", [128, 512], F32), "scol": ("sbuf", [128, 4], F32), "k1": ("sbuf", [128, 512], F32),
-    "cmp": ("sbuf", [128, 2560], BF), "junk": ("sbuf", [128, 2560], BF), "cnt": ("sbuf", [128, 4], F32),
-    "scn": ("sbuf", [128, 128], BF), "rof": ("sbuf", [128, 4], U16),
+    "cmp": ("sbuf", [128, 2560], BF), "junk": ("sbuf", [128, 2560], BF),
+    "cna": ("sbuf", [128, 4], F32), "cnb": ("sbuf", [128, 4], F32), "cnc": ("sbuf", [128, 4], F32),
+    "scn": ("sbuf", [128, 384], BF), "rof": ("sbuf", [128, 4], U16),
     "win": ("sbuf", [128, 512], F32), "win2": ("sbuf", [128, 8, 32], F32), "tr": ("sbuf", [128, 8, 32], F32),
     "a0": ("sbuf", [128, 8], F32), "a1": ("sbuf", [128, 8], F32), "a2": ("sbuf", [128, 8], F32),
     "ofs": ("sbuf", [128, 32], U16),
@@ -89,7 +90,7 @@ def rank_program(g, core, T, topo):
         queues[q].dma_start(out, in_).then_inc(T.sem[sem], 16)
         return (sem, 16)
 
-    V, S, TE, Y = g.vector, g.scalar, g.tensor, g.sync
+    V, S, TE = g.vector, g.scalar, g.tensor
     me = rank
     mates = [s for s in range(NR) if s != me and topo.chip(T.cores[s]) == topo.chip(core)]
     late = [s for s in range(NR) if s != me and s not in mates]
@@ -105,10 +106,10 @@ def rank_program(g, core, T, topo):
     k_win = did("v", V.memset(T.win[:, 0:128], 0.0))
     k_tab = did("v", V.memset(T.tab[:, 0:ZB], 0.0))
     k_pi = did("g", g.iota(T.pi[:, :], [[0, 32]], 0, 1))
-    k_ji = did("g", g.iota(T.ji[:, :], [[1, 512]], 0, 0))
-    k_gi = did("g", g.iota(T.gi[:, :], [[128, 4], [1, 16]], 0, 0, allow_small_or_imprecise_dtypes=True))
+    k_m4 = did("g", g.iota(T.m4[:, :], [[0, 128], [1, 4]], 0, 0, allow_small_or_imprecise_dtypes=True))
     need("g", k_ones)
     k_ew = did("g", g.affine_select(T.ew[:, :], T.ones[:, :], [[1, 520]], A.is_equal, 0.0, -4, -4))
+    k_gi = did("g", g.iota(T.gi[:, :], [[128, 4], [1, 16]], 0, 0, allow_small_or_imprecise_dtypes=True))
     k_jf = did("g", g.iota(T.jf[:, :], [[1, 512]], 0, 0, allow_small_or_imprecise_dtypes=True))
 
     need("v", k_pi)
@@ -119,84 +120,93 @@ def rank_program(g, core, T, topo):
     k_uof = did("v", V.tensor_copy(T.uof[:, :], T.t3[:, :]))
     k_tcol = did("v", V.tensor_copy(T.tcol[:, 0:1], T.t3[:, 0:1]))
     need("v", c3)
-    k_p4 = did("v", V.tensor_copy(T.p4f[:, 0:1], T.p4i[:, 0:1]))
+    k_p4 = did("v", V.tensor_scalar(T.p4n[:, 0:1], T.p4i[:, 0:1], -1.0, None, A.mult))
     k_p16 = did("v", V.tensor_copy(T.p16f[:, 0:1], T.p16i[:, 0:1]))
     need("v", k_tcol)
     k_tz = did("v", V.tensor_scalar(T.tz[:, 0:1], T.tcol[:, 0:1], float(ZB), None, A.add))
-    need("v", k_ji)
-    k_m4 = did("v", V.tensor_scalar(T.m4[:, :], T.ji[:, :], 3, None, A.bitwise_and))
-    need("v", k_m4, k_p4)
-    k_mk4 = did("v", V.tensor_scalar(T.mk4[:, :], T.m4[:, :], T.p4f[:, 0:1], None, A.is_equal))
     need("v", k_uof, ldu)
     k_ur = did("v", V.tensor_copy(T.urep[:, :], T.u4[:, 0:4].indirect(T.uof[:, :])))
     need("v", k_ur)
     k_uq = did("v", V.quantize_mx(T.uq[:, :], T.us[:, :], T.urep[:, :]))
-    k_rst = did("v", V.tensor_scalar(T.rst[:, :], T.m4[:, :], 0.0, None, A.not_equal))
+    k_eq = {}
+    need("v", k_ew)
+    for b in range(4):
+        c = slice(128 * b, 128 * b + 128)
+        k_eq[b] = did("v", V.quantize_mx(T.eq[:, c], T.es[:, c], T.ew[:, 4 - b:516 - b]))
     need("v", k_gi, k_p16)
     k_gd = did("v", V.tensor_scalar(T.gd[:, :], T.gi[:, :], T.p16f[:, 0:1], None, A.add))
 
-    need("s", k_jf, k_tz)
-    k_dat = did("s", S.activation(T.dat[:, :], T.jf[:, :], F.Identity, bias=T.tz[:, 0:1], scale=4.0))
-    k_pw = did("s", S.activation(T.pw[:, :], T.jf[:, :], F.Identity, bias=T.tcol[:, 0:1], scale=0.0))
+    need("s", k_m4, k_p4)
+    k_md = did("s", S.activation(T.m4d[:, :], T.m4[:, :], F.Abs, bias=T.p4n[:, 0:1]))
+    k_rst = did("s", S.activation(T.rst[:, :], T.m4[:, :], F.Sign))
+    need("s", k_md)
+    k_mk4 = did("s", S.activation(T.mk4[:, :], T.m4d[:, :], F.Relu, bias=1.0, scale=-1.0))
+    need("s", k_tz)
+    k_pw = did("s", S.activation(T.pw[:, :], T.m4[:, :], F.Identity, bias=T.tcol[:, 0:1], scale=0.0))
 
-    k_gq, k_row, k_col, k_abs = {}, {}, {}, {}
+    k_gq, k_abs, k_scol, k_k1 = {}, {}, {}, {}
     for a in range(4):
         need("v", ld[a])
         c = slice(128 * a, 128 * a + 128)
         k_gq[a] = did("v", V.quantize_mx(T.gq[:, c], T.gs[:, c], T.grt[:, 512 * a:512 * a + 512]))
         need("t", k_uq, k_gq[a])
         o = slice(512 * a, 512 * a + 128)
-        k_row[a] = did("t", TE.matmul_mx(T.psa[:, o], T.uq[:, :], T.us[:, :], T.gq[:, c], T.gs[:, c], True, True))
-        k_col[a] = did("t", TE.matmul_mx(T.psb[:, o], T.gq[:, c], T.gs[:, c], T.uq[:, :], T.us[:, :], True, True))
-        need("s", k_row[a])
+        k_row = did("t", TE.matmul_mx(T.psa[:, o], T.uq[:, :], T.us[:, :], T.gq[:, c], T.gs[:, c], True, True))
+        k_col = did("t", TE.matmul_mx(T.psb[:, o], T.gq[:, c], T.gs[:, c], T.uq[:, :], T.us[:, :], True, True))
+        need("s", k_row)
         k_abs[a] = did("s", S.activation(T.sab[:, c], T.psa[:, o], F.Abs))
-    need("s", k_col[3])
-    k_scol = did("s", S.activation(T.scol[:, 0:4], T.psb[:, 0:1537:512], F.Abs))
-    need("g", k_abs[3])
-    k_k1 = did("g", g.affine_select(T.k1[:, :], T.sab[:, :], [[0, 4], [-1, 128]], A.is_gt, -1.0, 0, 1))
-    k_eq = {}
-    need("v", k_ew)
-    for b in range(4):
-        c = slice(128 * b, 128 * b + 128)
-        k_eq[b] = did("v", V.quantize_mx(T.eq[:, c], T.es[:, c], T.ew[:, 4 - b:516 - b]))
+        need("s", k_col)
+        k_scol[a] = did("s", S.activation(T.scol[:, a:a + 1], T.psb[:, 512 * a:512 * a + 1], F.Abs))
+        need("g", k_abs[a])
+        k_k1[a] = did("g", g.affine_select(T.k1[:, c], T.sab[:, c], [[-1, 128]], A.is_gt, -1.0, 0, 1))
 
-    k_cmp = {}
-
-    def main(a):
-        sc, o, n = T.scol[:, a:a + 1], 640 * a, 128 * a
-        if n:
-            k_cmp[a, 0] = did("v", V.tensor_scalar(T.cmp[:, o:o + n], T.sab[:, 0:n], sc, None, A.is_ge))
-        k_cmp[a, 1] = did("v", V.tensor_scalar(T.cmp[:, o + n:o + 512], T.sab[:, n:512], sc, None, A.is_gt))
+    def against(a, lo, hi):
+        at = 640 * a + (lo if lo < 384 else lo + 128)
+        need("v", k_scol[a], k_abs[(hi - 1) // 128])
+        k, n = None, 128 * a
+        if lo < n:
+            m = min(n, hi)
+            k = did("v", V.tensor_scalar(T.cmp[:, at:at + m - lo], T.sab[:, lo:m], T.scol[:, a:a + 1], None, A.is_ge))
+        if n < hi:
+            m = max(n, lo)
+            k = did("v", V.tensor_scalar(T.cmp[:, at + m - lo:at + hi - lo], T.sab[:, m:hi], T.scol[:, a:a + 1], None, A.is_gt))
+        return k
 
     def ties(a):
-        need("v", k_k1)
-        k_cmp[a, 2] = did("v", V.tensor_scalar(T.cmp[:, 640 * a + 512:640 * a + 640], T.k1[:, 128 * a:128 * a + 128],
-                                               T.scol[:, a:a + 1], None, A.is_equal))
+        need("v", k_k1[a])
+        return did("v", V.tensor_scalar(T.cmp[:, 640 * a + 384:640 * a + 512], T.k1[:, 128 * a:128 * a + 128],
+                                        T.scol[:, a:a + 1], None, A.is_equal))
 
-    need("v", k_scol, k_abs[3])
-    main(0)
-    main(1)
-    ties(0)
-    ties(1)
-    main(2)
-    ties(2)
-    main(3)
-    ties(3)
-    k_cnt = {}
+    def total_of(a, lo, hi, out, k):
+        need("s", k)
+        o = slice(640 * a + lo, 640 * a + hi)
+        return did("s", S.activation(T.junk[:, o], T.cmp[:, o], F.Copy, accum_out=out[:, a:a + 1]))
+
     for a in range(3):
-        need("s", k_cmp[a, 2])
-        o = slice(640 * a, 640 * a + 640)
-        k_cnt[a] = did("s", S.activation(T.junk[:, o], T.cmp[:, o], F.Copy, accum_out=T.cnt[:, a:a + 1]))
-    need("s", k_cmp[3, 0])
-    k_cnt[3] = did("s", S.activation(T.junk[:, 1920:2304], T.cmp[:, 1920:2304], F.Copy, accum_out=T.cnt[:, 3:4]))
-    need("v", k_cmp[3, 2])
-    k_scn = did("v", V.tensor_tensor_scan(T.scn[:, :], T.cmp[:, 2304:2432], T.cmp[:, 2432:2560], 0.0, A.add, A.add))
-    need("v", k_cnt[2])
-    k_r0 = did("v", V.tensor_copy(T.rof[:, 0:3], T.cnt[:, 0:3]))
-    need("v", k_cnt[3], k_scn)
-    k_r1 = did("v", V.tensor_scalar(T.rof[:, 3:4], T.scn[:, 127:128], T.cnt[:, 3:4], None, A.add))
+        against(a, 0, 384)
+        k = ties(a)
+        k_ca = total_of(a, 0, 512, T.cna, k)
+    for a in range(3):
+        k = against(a, 384, 512)
+        k_cb = total_of(a, 512, 640, T.cnb, k)
+    k1 = against(3, 0, 384)
+    ties(3)
+    k2 = against(3, 384, 512)
+    need("v", k1)
+    did("v", V.tensor_tensor_scan(T.scn[:, 0:128], T.cmp[:, 1920:2048], T.cmp[:, 2048:2176], 0.0, A.add, A.add))
+    need("v", k2)
+    did("v", V.tensor_tensor_scan(T.scn[:, 128:256], T.cmp[:, 2176:2304], T.cmp[:, 2304:2432], 0.0, A.add, A.add))
+    k3 = did("v", V.tensor_tensor_scan(T.scn[:, 256:320], T.cmp[:, 2432:2496], T.cmp[:, 2496:2560], 0.0, A.add, A.add))
+    need("v", k_ca, k_cb)
+    k4 = did("v", V.tensor_tensor(T.cnc[:, 0:3], T.cna[:, 0:3], T.cnb[:, 0:3], A.add))
+    need("v", k3)
+    did("v", V.tensor_scalar(T.rof[:, 3:4], T.scn[:, 127:128], T.scn[:, 255:256], T.scn[:, 319:320], A.add, A.add))
+    need("v", k4)
+    k_r = did("v", V.tensor_copy(T.rof[:, 0:3], T.cnc[:, 0:3]))
+    need("s", k_jf, k_tz)
+    k_dat = did("s", S.activation(T.dat[:, :], T.jf[:, :], F.Identity, bias=T.tz[:, 0:1], scale=4.0))
 
-    need("v", k_r1, k_win, k_gd)
+    need("v", k_r, k_win, k_gd)
     k_w = did("v", V.tensor_copy(T.win[:, 0:512].indirect(T.rof[:, 0:4]), T.gd[:, :]))
     need("v", k_w)
     need("s", k_w)
@@ -260,6 +270,10 @@ def rank_program(g, core, T, topo):
     send(qs[me][:, :].bitcast(dt.uint8), qs[me][:, :].bitcast(dt.uint8), "ac%d" % me)
     send(ps[me][:, :], ps[me][:, :], "ac%d" % me)
 
+    x, y = late
+    order = [0, 1, 2, 3] if x else [1, 0, 2, 3]
+    place = {s: i for i, s in enumerate(order)}
+
     def decode(s, bank, *toks):
         need("t", k_eq[3], *toks)
         r = {}
@@ -269,14 +283,22 @@ def rank_program(g, core, T, topo):
         return r
 
     def column(s, b):
-        return T.tab[:, ZB + 512 * s + b:ZB + 512 * s + 512:4]
+        o = ZB + 512 * place[s]
+        return T.tab[:, o + b:o + 512:4]
+
+    def keep(s, bank, dec):
+        r = []
+        for b in range(4):
+            need("s", dec[b])
+            r.append(did("s", S.activation(column(s, b), bank[:, 512 * b:512 * b + 128], F.Copy)))
+        return r
 
     got = {s: ("ac%d" % s, 2 * narr[s]) for s in narr}
     heard = {s: ("al%d" % s, narr[s]) for s in narr}
     heard[me] = k_lst
     k_v = {}
     dec = decode(me, T.psa, k_q, k_abs[3])
-    need("t", k_scol)
+    need("t", k_scol[3])
     k_sc = did("t", TE.matmul_mx(T.psb[:, 0:128], T.uq[:, :], T.us[:, :], qs[me][:, :], ps[me][:, :], True, True))
     k_dif = {}
     for b in range(4):
@@ -287,10 +309,7 @@ def rank_program(g, core, T, topo):
     k_ers = did("v", V.tensor_copy(T.er32[:, 0:2048].indirect(T.ofs[:, 0:32]), T.dif[:, :]))
     need("y", k_ers)
     ends = [dma("y", "ster", T.er[:, :], T.er32[:, :])]
-    k_v[me] = []
-    for b in range(4):
-        need("s", k_dif[b])
-        k_v[me].append(did("s", S.activation(column(me, b), T.psa[:, 512 * b:512 * b + 128], F.Copy)))
+    k_v[me] = keep(me, T.psa, k_dif)
     need("s", k_sc)
     k_scb = did("s", S.activation(T.scb[:, :], T.psb[:, 0:128], F.Abs))
     need("y", k_scb)
@@ -298,70 +317,52 @@ def rank_program(g, core, T, topo):
 
     need("v", k_dat, k_pw, k_mk4)
     k_pv = k_sca = None
-    for s in range(NR):
+    for i, s in enumerate(order):
         need("v", heard[s])
-        if s:
+        if i:
             need("v", k_sca)
-            k_pv = did("v", V.tensor_tensor(T.pv[:, 128 * s - 128:128 * s], T.pw[:, 0:512].indirect(lists[s][:, 0:8]),
+            k_pv = did("v", V.tensor_tensor(T.pv[:, 128 * i - 128:128 * i], T.pw[:, 0:512].indirect(lists[s][:, 0:8]),
                                             T.mk4[:, 0:128], A.mult))
             need("v", k_pv)
-        k_sca = did("v", V.tensor_copy(T.pw[:, 0:512].indirect(lists[s][:, 0:8]), T.dat[:, 128 * s:128 * s + 128]))
-    need("v", k_pv, k_rst)
+        k_sca = did("v", V.tensor_copy(T.pw[:, 0:512].indirect(lists[s][:, 0:8]), T.dat[:, 128 * i:128 * i + 128]))
+    need("v", k_rst)
     k1 = did("v", V.tensor_tensor_scan(T.pvs[:, :], T.rst[:, 0:384], T.pv[:, :], 0.0, A.mult, A.add))
-    need("v", k_sca)
-    k2 = did("v", V.tensor_tensor(T.lw[:, :], T.pw[:, :], T.mk4[:, :], A.mult))
     need("v", k1)
     k_pof = did("v", V.tensor_copy(T.pof[:, :], T.pvs[:, 3:384:4]))
-    need("v", k2)
-    k3 = did("v", V.tensor_tensor_scan(T.lws[:, :], T.rst[:, :], T.lw[:, :], 0.0, A.mult, A.add))
-    need("v", k3)
-    k_lof = did("v", V.tensor_copy(T.lof[:, :], T.lws[:, 3:512:4]))
 
-    prev = [k_scb]
-    for s in mates:
-        dec = decode(s, T.psb, got[s], *prev)
-        k_v[s] = []
-        for b in range(4):
-            need("s", dec[b])
-            k_v[s].append(did("s", S.activation(column(s, b), T.psb[:, 512 * b:512 * b + 128], F.Copy)))
-        prev = k_v[s]
     k_nb = None
     for s in range(NR):
         need("s", heard[s])
         k_nb = did("s", S.activation(T.nbl[:, 128 * s:128 * s + 128], T.jf[:, 0:512].indirect(lists[s][:, 0:8]), F.Copy))
     need("y", k_nb)
     ends.append(dma("y", "stnb", T.nb[:, :], T.nbl[0:1, :]))
+    prev = [k_scb]
+    for s in mates:
+        dec = decode(s, T.psb, got[s], *prev)
+        k_v[s] = keep(s, T.psb, dec)
+        prev = k_v[s]
+    need("s", k_sca, k_mk4)
+    for i in range(4):
+        k2 = did("s", S.activation(T.lw[:, i:512:4], T.pw[:, i:512:4], F.Identity, scale=T.mk4[:, i:i + 1]))
 
-    x, y = late
     dx = decode(x, T.psa, got[x], *k_v[me])
     dy = decode(y, T.psb, got[y], *prev)
-    need("v", k_tab)
-    if x == 0:
-        k_v[x] = []
-        for b in (2, 3):
-            need("s", dx[b])
-            k_v[x].append(did("s", S.activation(column(x, b), T.psa[:, 512 * b:512 * b + 128], F.Copy)))
-        for b in (0, 1):
-            need("v", dx[b])
-            k_v[x].append(did("v", V.tensor_copy(column(x, b), T.psa[:, 512 * b:512 * b + 128])))
-    k_v[y] = []
+    need("v", k_tab, k_pof, *k_v[order[0]])
+    k_gs = did("v", V.tensor_copy(T.gsum[:, :], T.tab[:, 0:ZB + 512].indirect(T.pof[:, 0:32])))
+    need("v", k2)
+    k3 = did("v", V.tensor_tensor_scan(T.lws[:, :], T.rst[:, :], T.lw[:, :], 0.0, A.mult, A.add))
+    need("v", k3)
+    k_lof = did("v", V.tensor_copy(T.lof[:, :], T.lws[:, 3:512:4]))
+    need("v", k_gs)
+    total = list(k_v[order[0]])
     for b in range(4):
-        need("s", dy[b])
-        k_v[y].append(did("s", S.activation(column(y, b), T.psb[:, 512 * b:512 * b + 128], F.Copy)))
-    total = list(k_v[0]) if 0 in k_v else []
-    for s in range(1, NR):
-        need("v", k_pof, k_tab, *total)
-        window = T.tab[:, 0:ZB + 512 * s].indirect(T.pof[:, 32 * s - 32:32 * s])
-        if s == x:
-            k_gs = did("v", V.tensor_copy(T.gsum[:, :], window))
-            need("v", k_gs)
-            for b in range(4):
-                need("v", dx[b])
-                total.append(did("v", V.tensor_tensor(column(s, b), T.gsum[:, b:512:4], T.psa[:, 512 * b:512 * b + 128], A.add)))
-        else:
-            need("v", *k_v[s])
-            o = T.tab[:, ZB + 512 * s:ZB + 512 * s + 512]
-            total.append(did("v", V.tensor_tensor(o, window, o, A.add)))
+        need("v", dx[b])
+        total.append(did("v", V.tensor_tensor(column(x, b), T.gsum[:, b:512:4], T.psa[:, 512 * b:512 * b + 128], A.add)))
+    k_v[y] = keep(y, T.psb, dy)
+    for i in (2, 3):
+        need("v", *k_v[order[i]], *total)
+        o = T.tab[:, ZB + 512 * i:ZB + 512 * i + 512]
+        total.append(did("v", V.tensor_tensor(o, T.tab[:, 0:ZB + 512 * i].indirect(T.pof[:, 32 * i - 32:32 * i]), o, A.add)))
     need("v", k_lof, *total)
     need("s", k_lof, k_tab, *total)
     for i in range(4):

@@ -3,35 +3,33 @@ from concourse.mybir import dt, AluOpType as A, ActivationFunctionType as F
 
 NR = 4
 K = 128
-ZB = 16
+ZB = 4
 TW = ZB + 512 * NR
 X4, U8, F32, BF, I32, U16 = "float8_e4m3fn_x4", "uint8", "float32", "bfloat16", "int32", "uint16"
 
 SCRATCH = {
     "u4": ("sbuf", [128, 16], BF), "grt": ("sbuf", [128, 2048], BF), "urep": ("sbuf", [128, 512], BF),
-    "sel": ("sbuf", [128, 512], BF), "ones": ("sbuf", [128, 520], BF), "ew": ("sbuf", [128, 520], BF),
+    "sel": ("sbuf", [128, 512], BF), "ones": ("sbuf", [128, 512], BF), "ew": ("sbuf", [128, 520], BF),
     "uq": ("sbuf", [128, 128], X4), "us": ("sbuf", [128, 128], U8),
     "gq": ("sbuf", [128, 512], X4), "gs": ("sbuf", [128, 512], U8),
     "eq": ("sbuf", [128, 512], X4), "es": ("sbuf", [128, 512], U8),
     "psa": ("psum", [128, 2048], F32), "psb": ("psum", [128, 2048], F32),
     "pi": ("sbuf", [128, 32], I32), "t3": ("sbuf", [128, 32], I32), "uof": ("sbuf", [128, 32], U16),
     "p4i": ("sbuf", [128, 8], I32), "p16i": ("sbuf", [128, 8], I32),
-    "tcol": ("sbuf", [128, 8], F32), "p4n": ("sbuf", [128, 8], F32), "p16f": ("sbuf", [128, 8], F32),
-    "tz": ("sbuf", [128, 8], F32),
-    "m4": ("sbuf", [128, 512], F32), "m4d": ("sbuf", [128, 512], F32), "jf": ("sbuf", [128, 512], F32),
-    "mk4": ("sbuf", [128, 512], F32), "rst": ("sbuf", [128, 512], F32),
-    "gi": ("sbuf", [128, 64], F32), "gd": ("sbuf", [128, 64], F32),
+    "p4n": ("sbuf", [128, 8], F32), "p16f": ("sbuf", [128, 8], F32), "tz": ("sbuf", [128, 8], F32),
+    "m4": ("sbuf", [128, 128], F32), "m4d": ("sbuf", [128, 128], F32), "mk4": ("sbuf", [128, 128], F32),
+    "rst": ("sbuf", [128, 512], BF), "gi": ("sbuf", [128, 64], BF), "gd": ("sbuf", [128, 64], BF),
     "sab": ("sbuf", [128, 512], F32), "scol": ("sbuf", [128, 4], F32), "k1": ("sbuf", [128, 512], F32),
-    "cmp": ("sbuf", [128, 2560], BF), "junk": ("sbuf", [128, 2560], BF),
-    "cna": ("sbuf", [128, 4], F32), "cnb": ("sbuf", [128, 4], F32), "cnc": ("sbuf", [128, 4], F32),
+    "cmp": ("sbuf", [128, 2560], BF), "junk": ("sbuf", [128, 2560], BF), "jnk2": ("sbuf", [128, 768], F32),
+    "cna": ("sbuf", [128, 4], F32), "cnb": ("sbuf", [128, 4], F32),
     "scn": ("sbuf", [128, 384], BF), "rof": ("sbuf", [128, 4], U16),
-    "win": ("sbuf", [128, 512], F32), "win2": ("sbuf", [128, 8, 32], F32), "tr": ("sbuf", [128, 8, 32], F32),
-    "a0": ("sbuf", [128, 8], F32), "a1": ("sbuf", [128, 8], F32), "a2": ("sbuf", [128, 8], F32),
+    "win": ("sbuf", [128, 512], BF), "win2": ("sbuf", [128, 8, 32], BF), "tr": ("sbuf", [128, 8, 32], BF),
+    "a0": ("sbuf", [128, 8], BF), "a1": ("sbuf", [128, 8], BF), "a2": ("sbuf", [128, 8], BF),
     "ofs": ("sbuf", [128, 32], U16),
     "er32": ("sbuf", [128, 2048], F32), "dif": ("sbuf", [128, 512], F32),
-    "tab": ("sbuf", [128, TW], F32), "pw": ("sbuf", [128, 512], F32), "dat": ("sbuf", [128, 512], F32),
-    "pv": ("sbuf", [128, 384], F32), "pvs": ("sbuf", [128, 384], F32), "pof": ("sbuf", [128, 96], U16),
-    "lw": ("sbuf", [128, 512], F32), "lws": ("sbuf", [128, 512], F32), "lof": ("sbuf", [128, 128], U16),
+    "tab": ("sbuf", [128, TW], F32), "pw": ("sbuf", [128, 512], BF), "dat": ("sbuf", [128, 512], BF),
+    "pv": ("sbuf", [128, 384], BF), "pvs": ("sbuf", [128, 384], BF), "pof": ("sbuf", [128, 96], U16),
+    "lw": ("sbuf", [128, 512], BF), "lws": ("sbuf", [128, 512], BF), "lof": ("sbuf", [128, 128], U16),
     "gsum": ("sbuf", [128, 512], F32), "accs": ("sbuf", [128, 2048], F32),
     "nbl": ("sbuf", [128, 512], F32), "scb": ("sbuf", [128, 128], F32),
 }
@@ -40,8 +38,10 @@ for _s in range(NR):
     SCRATCH["q%d" % _s] = ("sbuf", [128, 128], X4)
     SCRATCH["p%d" % _s] = ("sbuf", [128, 128], U8)
 
-SEMAPHORES = (["gp", "ve", "se", "te", "left", "ldu", "ster", "stnb", "stsc"]
-              + ["ld%d" % i for i in range(4)] + ["sta%d" % i for i in range(4)]
+PIECES = (544, 544, 480, 480)
+
+SEMAPHORES = (["gp", "ve", "se", "te", "left", "ldu", "lde", "ster", "stnb", "stsc"]
+              + ["ld%d" % i for i in range(4)] + ["sta%d" % i for i in range(len(PIECES))]
               + ["al%d" % i for i in range(NR)] + ["ac%d" % i for i in range(NR)])
 
 
@@ -55,10 +55,10 @@ def engines_of(src, cores, topo):
         n = len(e) // len(off)
         plan[c] = e[i * n:(i + 1) * n]
         used += plan[c]
-    for i, c in enumerate(on):
-        e = [x for x in topo.engines(src, c) if x not in used]
-        n = len(e) // len(on)
-        plan[c] = e[i * n:(i + 1) * n]
+    width = len(used) // len(off)
+    for c in on:
+        plan[c] = [x for x in topo.engines(src, c) if x not in used][:width]
+        used += plan[c]
     return plan
 
 
@@ -102,15 +102,15 @@ def rank_program(g, core, T, topo):
     for a in range(4):
         ld[a] = dma("s" if a % 2 == 0 else "y", "ld%d" % a, T.grt[:, 512 * a:512 * a + 512], T.gr[:, 512 * a:512 * a + 512])
 
-    k_ones = did("v", V.memset(T.ones[:, :], 1.0))
-    k_win = did("v", V.memset(T.win[:, 0:128], 0.0))
-    k_tab = did("v", V.memset(T.tab[:, 0:ZB], 0.0))
     k_pi = did("g", g.iota(T.pi[:, :], [[0, 32]], 0, 1))
-    k_m4 = did("g", g.iota(T.m4[:, :], [[0, 128], [1, 4]], 0, 0, allow_small_or_imprecise_dtypes=True))
-    need("g", k_ones)
-    k_ew = did("g", g.affine_select(T.ew[:, :], T.ones[:, :], [[1, 520]], A.is_equal, 0.0, -4, -4))
-    k_gi = did("g", g.iota(T.gi[:, :], [[128, 4], [1, 16]], 0, 0, allow_small_or_imprecise_dtypes=True))
-    k_jf = did("g", g.iota(T.jf[:, :], [[1, 512]], 0, 0, allow_small_or_imprecise_dtypes=True))
+    k_ew0 = did("v", V.memset(T.ew[:, :], 0.0))
+    k_ones = did("v", V.memset(T.ones[:, :], 1.0))
+    need("g", k_ew0, k_ones)
+    k_ew = did("g", g.affine_select(T.ew[:, 4:516:4], T.ones[:, 0:128], [[1, 128]], A.is_equal, 0.0, 0, -1))
+    k_m4 = did("g", g.iota(T.m4[:, :], [[0, 32], [1, 4]], 0, 0, allow_small_or_imprecise_dtypes=True))
+    k_gi = did("g", g.iota(T.gi[:, :], [[128, 4], [1, 16]], -256, 0, allow_small_or_imprecise_dtypes=True))
+    g.dma_start(T.er32[:, :], T.gr[:, :]).then_inc(T.sem.lde, 16)
+    k_er = ("lde", 16)
 
     need("v", k_pi)
     c1 = did("v", V.tensor_scalar(T.t3[:, :], T.pi[:, :], 3, None, A.bitwise_and))
@@ -118,37 +118,28 @@ def rank_program(g, core, T, topo):
     c3 = did("v", V.tensor_scalar(T.p16i[:, 0:1], T.pi[:, 0:1], 112, None, A.bitwise_and))
     need("v", c1)
     k_uof = did("v", V.tensor_copy(T.uof[:, :], T.t3[:, :]))
-    k_tcol = did("v", V.tensor_copy(T.tcol[:, 0:1], T.t3[:, 0:1]))
-    need("v", c3)
-    k_p4 = did("v", V.tensor_scalar(T.p4n[:, 0:1], T.p4i[:, 0:1], -1.0, None, A.mult))
-    k_p16 = did("v", V.tensor_copy(T.p16f[:, 0:1], T.p16i[:, 0:1]))
-    need("v", k_tcol)
-    k_tz = did("v", V.tensor_scalar(T.tz[:, 0:1], T.tcol[:, 0:1], float(ZB), None, A.add))
-    need("v", k_uof, ldu)
-    k_ur = did("v", V.tensor_copy(T.urep[:, :], T.u4[:, 0:4].indirect(T.uof[:, :])))
-    need("v", k_ur)
-    k_uq = did("v", V.quantize_mx(T.uq[:, :], T.us[:, :], T.urep[:, :]))
-    k_eq = {}
     need("v", k_ew)
+    k_eq = {}
     for b in range(4):
         c = slice(128 * b, 128 * b + 128)
         k_eq[b] = did("v", V.quantize_mx(T.eq[:, c], T.es[:, c], T.ew[:, 4 - b:516 - b]))
-    need("v", k_gi, k_p16)
-    k_gd = did("v", V.tensor_scalar(T.gd[:, :], T.gi[:, :], T.p16f[:, 0:1], None, A.add))
+    need("v", c3)
+    k_p4 = did("v", V.tensor_scalar(T.p4n[:, 0:1], T.p4i[:, 0:1], -1.0, None, A.mult))
 
-    need("s", k_m4, k_p4)
-    k_md = did("s", S.activation(T.m4d[:, :], T.m4[:, :], F.Abs, bias=T.p4n[:, 0:1]))
-    k_rst = did("s", S.activation(T.rst[:, :], T.m4[:, :], F.Sign))
-    need("s", k_md)
-    k_mk4 = did("s", S.activation(T.mk4[:, :], T.m4d[:, :], F.Relu, bias=1.0, scale=-1.0))
-    need("s", k_tz)
-    k_pw = did("s", S.activation(T.pw[:, :], T.m4[:, :], F.Identity, bias=T.tcol[:, 0:1], scale=0.0))
+    need("v", k_uof, ldu)
+    need("s", k_uof, ldu)
+    u1 = did("v", V.tensor_copy(T.urep[:, 0:256], T.u4[:, 0:4].indirect(T.uof[:, 0:16])))
+    u2 = did("s", S.activation(T.urep[:, 256:512], T.u4[:, 0:4].indirect(T.uof[:, 16:32]), F.Copy))
 
     k_gq, k_abs, k_scol, k_k1 = {}, {}, {}, {}
-    for a in range(4):
+
+    def codes(a):
         need("v", ld[a])
         c = slice(128 * a, 128 * a + 128)
         k_gq[a] = did("v", V.quantize_mx(T.gq[:, c], T.gs[:, c], T.grt[:, 512 * a:512 * a + 512]))
+
+    def score(a):
+        c = slice(128 * a, 128 * a + 128)
         need("t", k_uq, k_gq[a])
         o = slice(512 * a, 512 * a + 128)
         k_row = did("t", TE.matmul_mx(T.psa[:, o], T.uq[:, :], T.us[:, :], T.gq[:, c], T.gs[:, c], True, True))
@@ -159,6 +150,18 @@ def rank_program(g, core, T, topo):
         k_scol[a] = did("s", S.activation(T.scol[:, a:a + 1], T.psb[:, 512 * a:512 * a + 1], F.Abs))
         need("g", k_abs[a])
         k_k1[a] = did("g", g.affine_select(T.k1[:, c], T.sab[:, c], [[-1, 128]], A.is_gt, -1.0, 0, 1))
+
+    codes(0)
+    need("v", u1, u2)
+    k_uq = did("v", V.quantize_mx(T.uq[:, :], T.us[:, :], T.urep[:, :]))
+    for a in (1, 2, 3):
+        codes(a)
+    for a in range(4):
+        score(a)
+    k_win = did("v", V.memset(T.win[:, 0:128], 0.0))
+    k_p16 = did("v", V.tensor_copy(T.p16f[:, 0:1], T.p16i[:, 0:1]))
+    k_tz = did("v", V.tensor_scalar(T.tz[:, 0:1], T.t3[:, 0:1], 1024.0, None, A.add))
+    k_dat = did("g", g.iota(T.dat[:, :], [[1, 512]], -255, 0, allow_small_or_imprecise_dtypes=True))
 
     def against(a, lo, hi):
         at = 640 * a + (lo if lo < 384 else lo + 128)
@@ -177,79 +180,83 @@ def rank_program(g, core, T, topo):
         return did("v", V.tensor_scalar(T.cmp[:, 640 * a + 384:640 * a + 512], T.k1[:, 128 * a:128 * a + 128],
                                         T.scol[:, a:a + 1], None, A.is_equal))
 
-    def total_of(a, lo, hi, out, k):
-        need("s", k)
-        o = slice(640 * a + lo, 640 * a + hi)
-        return did("s", S.activation(T.junk[:, o], T.cmp[:, o], F.Copy, accum_out=out[:, a:a + 1]))
+    k_ca = {}
 
+    def first_sum(a, k):
+        need("s", k)
+        o = slice(640 * a, 640 * a + 384)
+        k_ca[a] = did("s", S.activation(T.junk[:, o], T.cmp[:, o], F.Copy, scale=1.0 / 256, accum_out=T.cna[:, a:a + 1]))
+
+    def last_sum(a, k):
+        need("s", k, k_ca[a])
+        return did("s", S.activation(T.jnk2[:, 256 * a:256 * a + 256], T.cmp[:, 640 * a + 384:640 * a + 640], F.Identity,
+                                     bias=T.cna[:, a:a + 1], accum_out=T.cnb[:, a:a + 1]))
+
+    against(0, 0, 256)
+    against(1, 0, 256)
+    k = against(0, 256, 384)
+    first_sum(0, k)
+    k = against(1, 256, 384)
+    first_sum(1, k)
+    k = against(2, 0, 384)
+    first_sum(2, k)
     for a in range(3):
-        against(a, 0, 384)
-        k = ties(a)
-        k_ca = total_of(a, 0, 512, T.cna, k)
-    for a in range(3):
+        ties(a)
         k = against(a, 384, 512)
-        k_cb = total_of(a, 512, 640, T.cnb, k)
+        k_cb = last_sum(a, k)
     k1 = against(3, 0, 384)
     ties(3)
     k2 = against(3, 384, 512)
+    need("v", k_gi, k_p16)
+    k_gd = did("v", V.tensor_scalar(T.gd[:, :], T.gi[:, :], T.p16f[:, 0:1], None, A.add))
     need("v", k1)
     did("v", V.tensor_tensor_scan(T.scn[:, 0:128], T.cmp[:, 1920:2048], T.cmp[:, 2048:2176], 0.0, A.add, A.add))
     need("v", k2)
     did("v", V.tensor_tensor_scan(T.scn[:, 128:256], T.cmp[:, 2176:2304], T.cmp[:, 2304:2432], 0.0, A.add, A.add))
     k3 = did("v", V.tensor_tensor_scan(T.scn[:, 256:320], T.cmp[:, 2432:2496], T.cmp[:, 2496:2560], 0.0, A.add, A.add))
-    need("v", k_ca, k_cb)
-    k4 = did("v", V.tensor_tensor(T.cnc[:, 0:3], T.cna[:, 0:3], T.cnb[:, 0:3], A.add))
+    need("v", k_cb)
+    did("v", V.tensor_copy(T.rof[:, 0:3], T.cnb[:, 0:3]))
     need("v", k3)
-    did("v", V.tensor_scalar(T.rof[:, 3:4], T.scn[:, 127:128], T.scn[:, 255:256], T.scn[:, 319:320], A.add, A.add))
-    need("v", k4)
-    k_r = did("v", V.tensor_copy(T.rof[:, 0:3], T.cnc[:, 0:3]))
-    need("s", k_jf, k_tz)
-    k_dat = did("s", S.activation(T.dat[:, :], T.jf[:, :], F.Identity, bias=T.tz[:, 0:1], scale=4.0))
+    k_r = did("v", V.tensor_scalar(T.rof[:, 3:4], T.scn[:, 127:128], T.scn[:, 255:256], T.scn[:, 319:320], A.add, A.add))
 
     need("v", k_r, k_win, k_gd)
     k_w = did("v", V.tensor_copy(T.win[:, 0:512].indirect(T.rof[:, 0:4]), T.gd[:, :]))
     need("v", k_w)
-    need("s", k_w)
-    d1 = did("v", V.tensor_copy(T.win2[:, :, 0:16], T.win[:, 0:128]))
-    d2 = did("s", S.activation(T.win2[:, :, 16:32], T.win[:, 0:128], F.Copy))
-    need("v", d1, d2)
+    did("v", V.tensor_copy(T.win2[:, :, 0:16], T.win[:, 0:128]))
+    d2 = did("v", V.tensor_copy(T.win2[:, :, 16:32], T.win[:, 0:128]))
+    need("v", d2)
     k_tr = did("v", V.transpose(T.tr[:, :, :], T.win2[:, :, :]))
     need("v", k_tr)
     k_a0 = did("v", V.tensor_tensor(T.a0[:, :], T.tr[:, :, 0], T.tr[:, :, 16], A.add))
     need("v", k_a0)
-    for h in range(2):
-        k_a1 = did("v", V.tensor_tensor(T.a1[64 * h:64 * h + 64, :], T.a0[0:64, :], T.a0[64:128, :], A.add))
+    k_a1 = did("v", V.tensor_tensor(T.a1[0:64, :], T.a0[0:64, :], T.a0[64:128, :], A.add))
     need("v", k_a1)
     for b in range(4):
-        h = 64 * (b // 2)
-        k_a2 = did("v", V.tensor_tensor(T.a2[32 * b:32 * b + 32, :], T.a1[h:h + 32, :], T.a1[h + 32:h + 64, :], A.add))
+        k_a2 = did("v", V.tensor_tensor(T.a2[32 * b:32 * b + 32, :], T.a1[0:32, :], T.a1[32:64, :], A.add))
     lists = [T["lst%d" % s] for s in range(NR)]
     qs = [T["q%d" % s] for s in range(NR)]
     ps = [T["p%d" % s] for s in range(NR)]
     need("v", k_a2)
-    k_lst = did("v", V.tensor_copy(lists[me][:, :], T.a2[:, :]))
+    k_lst = did("v", V.tensor_scalar(lists[me][:, :], T.a2[:, :], 256.0, None, A.add))
     k_of = {}
     for t in (2, 3, 0, 1):
-        k_of[t] = did("v", V.tensor_scalar(T.ofs[:, 8 * t:8 * t + 8], T.a2[:, :], 4.0, float(t), A.mult, A.add))
+        k_of[t] = did("v", V.tensor_scalar(T.ofs[:, 8 * t:8 * t + 8], T.a2[:, :], 4.0, 1024.0 + t, A.mult, A.add))
     k_sel = {}
     for t in (0, 1):
         need("v", k_of[t])
         k_sel[t] = did("v", V.tensor_copy(T.sel[:, t:512:4], T.grt[:, 0:2048].indirect(T.ofs[:, 8 * t:8 * t + 8])))
-
-    k_er = {}
-
-    def widen(a):
-        o = slice(512 * a, 512 * a + 512)
-        need("s", ld[a])
-        k_er[a] = did("s", S.activation(T.er32[:, o], T.grt[:, o], F.Copy))
-
-    widen(0)
-    widen(1)
+    need("s", k_m4, k_p4)
+    k_md = did("s", S.activation(T.m4d[:, :], T.m4[:, :], F.Abs, bias=T.p4n[:, 0:1]))
+    did("s", S.activation(T.pw[:, :], T.ones[:, :], F.Copy, scale=-256.0))
+    did("s", S.activation(T.rst[:, :], T.ones[:, :], F.Copy))
+    need("s", k_md)
+    did("s", S.activation(T.mk4[:, :], T.m4d[:, :], F.Relu, bias=1.0, scale=-1.0))
+    k_tab = did("s", S.activation(T.tab[:, 0:ZB], T.ones[:, 0:ZB], F.Copy, scale=0.0))
+    need("s", k_tab)
+    k_rst = did("s", S.activation(T.rst[:, 0:512:4], T.ones[:, 0:128], F.Copy, scale=0.0))
     for t in (2, 3):
         need("s", k_of[t])
         k_sel[t] = did("s", S.activation(T.sel[:, t:512:4], T.grt[:, 0:2048].indirect(T.ofs[:, 8 * t:8 * t + 8]), F.Copy))
-    widen(2)
-    widen(3)
     need("v", k_sel[1], k_sel[3])
     k_q = did("v", V.quantize_mx(qs[me][:, :], ps[me][:, :], T.sel[:, :]))
 
@@ -297,83 +304,133 @@ def rank_program(g, core, T, topo):
     heard = {s: ("al%d" % s, narr[s]) for s in narr}
     heard[me] = k_lst
     k_v = {}
+
+    last = [k_rst]
+
+    def enter(i):
+        need("v", heard[order[i]], k_dat, *last)
+        last[:] = [did("v", V.tensor_copy(T.pw[:, 0:512].indirect(lists[order[i]][:, 0:8]), T.dat[:, 128 * i:128 * i + 128]))]
+
+    def lookup(i):
+        need("v", heard[order[i]], *last)
+        last[:] = [did("v", V.tensor_tensor(T.pv[:, 128 * i - 128:128 * i], T.pw[:, 0:512].indirect(lists[order[i]][:, 0:8]),
+                                            T.mk4[:, 0:128], A.mult))]
+        return last[0]
+
+    def unfold(out, src, n, k):
+        need("v", k, k_rst)
+        return did("v", V.tensor_tensor_scan(out, T.rst[:, 0:n], src, 0.0, A.mult, A.add))
+
+    def offsets(out, src, k):
+        need("v", k, k_tz)
+        return did("v", V.tensor_scalar(out, src, 4.0, T.tz[:, 0:1], A.mult, A.add))
+
     dec = decode(me, T.psa, k_q, k_abs[3])
     need("t", k_scol[3])
     k_sc = did("t", TE.matmul_mx(T.psb[:, 0:128], T.uq[:, :], T.us[:, :], qs[me][:, :], ps[me][:, :], True, True))
+    if order[0] == me:
+        enter(0)
     k_dif = {}
     for b in range(4):
         need("v", dec[b])
         k_dif[b] = did("v", V.tensor_tensor(T.dif[:, 128 * b:128 * b + 128], T.sel[:, b:512:4],
                                             T.psa[:, 512 * b:512 * b + 128], A.subtract))
-    need("v", k_er[3], *k_dif.values())
-    k_ers = did("v", V.tensor_copy(T.er32[:, 0:2048].indirect(T.ofs[:, 0:32]), T.dif[:, :]))
-    need("y", k_ers)
+    k_ers = [k_er]
+
+    def place_er(h):
+        need("v", k_dif[2 * h + 1], *k_ers)
+        k_ers[:] = [did("v", V.tensor_copy(T.er32[:, 0:2048].indirect(T.ofs[:, 16 * h:16 * h + 16]),
+                                           T.dif[:, 256 * h:256 * h + 256]))]
+
+    place_er(0)
+    if order[0] != me:
+        enter(0)
+    place_er(1)
+    kp1 = lookup(1)
+    need("y", *k_ers)
     ends = [dma("y", "ster", T.er[:, :], T.er32[:, :])]
+    enter(1)
+    ku1 = unfold(T.pvs[:, 0:128], T.pv[:, 0:128], 128, kp1)
+    lookup(2)
+    k_pof1 = offsets(T.pof[:, 0:32], T.pvs[:, 3:128:4], ku1)
+    enter(2)
+    kp3 = lookup(3)
+    enter(3)
+    k_places = last[0]
+    ku2 = unfold(T.pvs[:, 128:384], T.pv[:, 128:384], 256, kp3)
+    k_pof = offsets(T.pof[:, 32:96], T.pvs[:, 131:384:4], ku2)
+
     k_v[me] = keep(me, T.psa, k_dif)
     need("s", k_sc)
     k_scb = did("s", S.activation(T.scb[:, :], T.psb[:, 0:128], F.Abs))
     need("y", k_scb)
     ends.append(dma("y", "stsc", T.sc[:, :], T.scb[0:1, :]))
-
-    need("v", k_dat, k_pw, k_mk4)
-    k_pv = k_sca = None
-    for i, s in enumerate(order):
-        need("v", heard[s])
-        if i:
-            need("v", k_sca)
-            k_pv = did("v", V.tensor_tensor(T.pv[:, 128 * i - 128:128 * i], T.pw[:, 0:512].indirect(lists[s][:, 0:8]),
-                                            T.mk4[:, 0:128], A.mult))
-            need("v", k_pv)
-        k_sca = did("v", V.tensor_copy(T.pw[:, 0:512].indirect(lists[s][:, 0:8]), T.dat[:, 128 * i:128 * i + 128]))
-    need("v", k_rst)
-    k1 = did("v", V.tensor_tensor_scan(T.pvs[:, :], T.rst[:, 0:384], T.pv[:, :], 0.0, A.mult, A.add))
-    need("v", k1)
-    k_pof = did("v", V.tensor_copy(T.pof[:, :], T.pvs[:, 3:384:4]))
-
-    k_nb = None
-    for s in range(NR):
-        need("s", heard[s])
-        k_nb = did("s", S.activation(T.nbl[:, 128 * s:128 * s + 128], T.jf[:, 0:512].indirect(lists[s][:, 0:8]), F.Copy))
-    need("y", k_nb)
-    ends.append(dma("y", "stnb", T.nb[:, :], T.nbl[0:1, :]))
     prev = [k_scb]
+
+    def gather_first():
+        need("s", k_tab, k_pof1, *k_v[order[0]])
+        return did("s", S.activation(T.gsum[:, :], T.tab[:, 0:ZB + 512].indirect(T.pof[:, 0:32]), F.Copy))
+
+    if order[0] == me:
+        k_gs = gather_first()
     for s in mates:
         dec = decode(s, T.psb, got[s], *prev)
         k_v[s] = keep(s, T.psb, dec)
         prev = k_v[s]
-    need("s", k_sca, k_mk4)
-    for i in range(4):
-        k2 = did("s", S.activation(T.lw[:, i:512:4], T.pw[:, i:512:4], F.Identity, scale=T.mk4[:, i:i + 1]))
+    if order[0] != me:
+        k_gs = gather_first()
+
+    def mask():
+        need("s", k_places, k_rst)
+        for i in range(4):
+            k = did("s", S.activation(T.lw[:, i:512:4], T.pw[:, i:512:4], F.Identity, scale=T.mk4[:, i:i + 1]))
+        return k
 
     dx = decode(x, T.psa, got[x], *k_v[me])
     dy = decode(y, T.psb, got[y], *prev)
-    need("v", k_tab, k_pof, *k_v[order[0]])
-    k_gs = did("v", V.tensor_copy(T.gsum[:, :], T.tab[:, 0:ZB + 512].indirect(T.pof[:, 0:32])))
-    need("v", k2)
-    k3 = did("v", V.tensor_tensor_scan(T.lws[:, :], T.rst[:, :], T.lw[:, :], 0.0, A.mult, A.add))
-    need("v", k3)
-    k_lof = did("v", V.tensor_copy(T.lof[:, :], T.lws[:, 3:512:4]))
+    early = order[2] != y
+    if early:
+        k_lw = mask()
+    k_v[y] = keep(y, T.psb, dy)
+    if not early:
+        k_lw = mask()
     need("v", k_gs)
     total = list(k_v[order[0]])
     for b in range(4):
         need("v", dx[b])
         total.append(did("v", V.tensor_tensor(column(x, b), T.gsum[:, b:512:4], T.psa[:, 512 * b:512 * b + 128], A.add)))
-    k_v[y] = keep(y, T.psb, dy)
+    if early:
+        ku = unfold(T.lws[:, :], T.lw[:, :], 512, k_lw)
     for i in (2, 3):
-        need("v", *k_v[order[i]], *total)
+        need("v", k_pof, *k_v[order[i]], *total)
         o = T.tab[:, ZB + 512 * i:ZB + 512 * i + 512]
         total.append(did("v", V.tensor_tensor(o, T.tab[:, 0:ZB + 512 * i].indirect(T.pof[:, 32 * i - 32:32 * i]), o, A.add)))
-    need("v", k_lof, *total)
+        if i == 2 and early:
+            k_lof = offsets(T.lof[:, :], T.lws[:, 3:512:4], ku)
+        if i == 2 and not early:
+            ku = unfold(T.lws[:, :], T.lw[:, :], 512, k_lw)
+    if not early:
+        k_lof = offsets(T.lof[:, :], T.lws[:, 3:512:4], ku)
+    k_nb = None
+    for s in range(NR):
+        need("s", heard[s], k_dat)
+        k_nb = did("s", S.activation(T.nbl[:, 128 * s:128 * s + 128], T.dat[:, 0:512].indirect(lists[s][:, 0:8]), F.Copy,
+                                     bias=255.0))
+    need("y", k_nb)
+    ends.append(dma("y", "stnb", T.nb[:, :], T.nbl[0:1, :]))
+    need("v", k_lof, k_tab, *total)
     need("s", k_lof, k_tab, *total)
-    for i in range(4):
-        o = T.accs[:, 512 * i:512 * i + 512]
-        window = T.tab[:, 0:TW].indirect(T.lof[:, 32 * i:32 * i + 32])
+    at = 0
+    for i, n in enumerate(PIECES):
+        o = T.accs[:, at:at + n]
+        window = T.tab[:, 0:TW].indirect(T.lof[:, at // 16:(at + n) // 16])
         if i % 2 == 0:
             k = did("v", V.tensor_copy(o, window))
         else:
             k = did("s", S.activation(o, window, F.Copy))
         need("y", k)
-        ends.append(dma("y", "sta%d" % i, T.acc[:, 512 * i:512 * i + 512], o))
+        ends.append(dma("y", "sta%d" % i, T.acc[:, at:at + n], o))
+        at += n
 
     need("y", *ends)
     need("g", ("left", sent[0]), *[(sem, count[sem]) for sem in ("gp", "ve", "se", "te")])

from concourse.bass import DstId, RemoteDMATransfer
from concourse.mybir import dt, AluOpType as A, ActivationFunctionType as F

NR = 4
K = 128
ZB = 4
TW = ZB + 512 * NR
X4, U8, F32, BF, I32, U16 = "float8_e4m3fn_x4", "uint8", "float32", "bfloat16", "int32", "uint16"

SCRATCH = {
    "u4": ("sbuf", [128, 16], BF), "grt": ("sbuf", [128, 2048], BF), "urep": ("sbuf", [128, 512], BF),
    "sel": ("sbuf", [128, 512], BF), "ones": ("sbuf", [128, 512], BF), "ew": ("sbuf", [128, 520], BF),
    "uq": ("sbuf", [128, 128], X4), "us": ("sbuf", [128, 128], U8),
    "gq": ("sbuf", [128, 512], X4), "gs": ("sbuf", [128, 512], U8),
    "eq": ("sbuf", [128, 512], X4), "es": ("sbuf", [128, 512], U8),
    "psa": ("psum", [128, 2048], F32), "psb": ("psum", [128, 2048], F32),
    "pi": ("sbuf", [128, 32], I32), "t3": ("sbuf", [128, 32], I32), "uof": ("sbuf", [128, 32], U16),
    "p4i": ("sbuf", [128, 8], I32), "p16i": ("sbuf", [128, 8], I32),
    "p4n": ("sbuf", [128, 8], F32), "p16f": ("sbuf", [128, 8], F32), "tz": ("sbuf", [128, 8], F32),
    "m4": ("sbuf", [128, 128], F32), "m4d": ("sbuf", [128, 128], F32), "mk4": ("sbuf", [128, 128], F32),
    "rst": ("sbuf", [128, 512], BF), "gi": ("sbuf", [128, 64], BF), "gd": ("sbuf", [128, 64], BF),
    "sab": ("sbuf", [128, 512], F32), "scol": ("sbuf", [128, 4], F32), "k1": ("sbuf", [128, 512], F32),
    "cmp": ("sbuf", [128, 2560], BF), "junk": ("sbuf", [128, 2560], BF), "jnk2": ("sbuf", [128, 768], F32),
    "cna": ("sbuf", [128, 4], F32), "cnb": ("sbuf", [128, 4], F32),
    "scn": ("sbuf", [128, 384], BF), "rof": ("sbuf", [128, 4], U16),
    "win": ("sbuf", [128, 512], BF), "win2": ("sbuf", [128, 8, 32], BF), "tr": ("sbuf", [128, 8, 32], BF),
    "a0": ("sbuf", [128, 8], BF), "a1": ("sbuf", [128, 8], BF), "a2": ("sbuf", [128, 8], BF),
    "ofs": ("sbuf", [128, 32], U16),
    "er32": ("sbuf", [128, 2048], F32), "dif": ("sbuf", [128, 512], F32),
    "tab": ("sbuf", [128, TW], F32), "pw": ("sbuf", [128, 512], BF), "dat": ("sbuf", [128, 512], BF),
    "pv": ("sbuf", [128, 384], BF), "pvs": ("sbuf", [128, 384], BF), "pof": ("sbuf", [128, 96], U16),
    "lw": ("sbuf", [128, 512], BF), "lws": ("sbuf", [128, 512], BF), "lof": ("sbuf", [128, 128], U16),
    "gsum": ("sbuf", [128, 512], F32), "accs": ("sbuf", [128, 2048], F32),
    "nbl": ("sbuf", [128, 512], F32), "scb": ("sbuf", [128, 128], F32),
}
for _s in range(NR):
    SCRATCH["lst%d" % _s] = ("sbuf", [128, 8], U16)
    SCRATCH["q%d" % _s] = ("sbuf", [128, 128], X4)
    SCRATCH["p%d" % _s] = ("sbuf", [128, 128], U8)

PIECES = (544, 544, 480, 480)

SEMAPHORES = (["gp", "ve", "se", "te", "left", "ldu", "lde", "ster", "stnb", "stsc"]
              + ["ld%d" % i for i in range(4)] + ["sta%d" % i for i in range(len(PIECES))]
              + ["al%d" % i for i in range(NR)] + ["ac%d" % i for i in range(NR)])


def engines_of(src, cores, topo):
    dsts = [c for c in cores if c != src]
    off = [c for c in dsts if topo.chip(c) != topo.chip(src)]
    on = [c for c in dsts if c not in off]
    plan, used = {}, []
    for i, c in enumerate(off):
        e = topo.engines(src, c)
        n = len(e) // len(off)
        plan[c] = e[i * n:(i + 1) * n]
        used += plan[c]
    width = len(used) // len(off)
    for c in on:
        plan[c] = [x for x in topo.engines(src, c) if x not in used][:width]
        used += plan[c]
    return plan


def rank_program(g, core, T, topo):
    rank = T.rank_of(core)
    if rank is None:
        return
    queues = {"g": g, "v": g.vector, "s": g.scalar, "t": g.tensor, "y": g.sync}
    count = {"gp": 0, "ve": 0, "se": 0, "te": 0}
    own = {"g": "gp", "v": "ve", "s": "se", "t": "te"}
    seen = {}

    def need(q, *toks):
        best = {}
        for tk in toks:
            best[tk[0]] = max(best.get(tk[0], 0), tk[1])
        for sem in best:
            if seen.get((q, sem), 0) < best[sem]:
                queues[q].wait_ge(T.sem[sem], best[sem])
                seen[(q, sem)] = best[sem]

    def did(q, ins):
        sem = own[q]
        ins.then_inc(T.sem[sem], 1)
        count[sem] += 1
        return (sem, count[sem])

    def dma(q, sem, out, in_):
        queues[q].dma_start(out, in_).then_inc(T.sem[sem], 16)
        return (sem, 16)

    V, S, TE = g.vector, g.scalar, g.tensor
    me = rank
    mates = [s for s in range(NR) if s != me and topo.chip(T.cores[s]) == topo.chip(core)]
    late = [s for s in range(NR) if s != me and s not in mates]
    plan = engines_of(core, T.cores, topo)
    narr = {s: len(engines_of(T.cores[s], T.cores, topo)[core]) for s in range(NR) if s != me}

    ldu = dma("y", "ldu", T.u4[:, 0:4], T.u[:, 0:4])
    ld = {}
    for a in range(4):
        ld[a] = dma("s" if a % 2 == 0 else "y", "ld%d" % a, T.grt[:, 512 * a:512 * a + 512], T.gr[:, 512 * a:512 * a + 512])

    k_pi = did("g", g.iota(T.pi[:, :], [[0, 32]], 0, 1))
    k_ew0 = did("v", V.memset(T.ew[:, :], 0.0))
    k_ones = did("v", V.memset(T.ones[:, :], 1.0))
    need("g", k_ew0, k_ones)
    k_ew = did("g", g.affine_select(T.ew[:, 4:516:4], T.ones[:, 0:128], [[1, 128]], A.is_equal, 0.0, 0, -1))
    k_m4 = did("g", g.iota(T.m4[:, :], [[0, 32], [1, 4]], 0, 0, allow_small_or_imprecise_dtypes=True))
    k_gi = did("g", g.iota(T.gi[:, :], [[128, 4], [1, 16]], -256, 0, allow_small_or_imprecise_dtypes=True))
    g.dma_start(T.er32[:, :], T.gr[:, :]).then_inc(T.sem.lde, 16)
    k_er = ("lde", 16)

    need("v", k_pi)
    c1 = did("v", V.tensor_scalar(T.t3[:, :], T.pi[:, :], 3, None, A.bitwise_and))
    c2 = did("v", V.tensor_scalar(T.p4i[:, 0:1], T.pi[:, 0:1], 2, 3, A.arith_shift_right, A.bitwise_and))
    c3 = did("v", V.tensor_scalar(T.p16i[:, 0:1], T.pi[:, 0:1], 112, None, A.bitwise_and))
    need("v", c1)
    k_uof = did("v", V.tensor_copy(T.uof[:, :], T.t3[:, :]))
    need("v", k_ew)
    k_eq = {}
    for b in range(4):
        c = slice(128 * b, 128 * b + 128)
        k_eq[b] = did("v", V.quantize_mx(T.eq[:, c], T.es[:, c], T.ew[:, 4 - b:516 - b]))
    need("v", c3)
    k_p4 = did("v", V.tensor_scalar(T.p4n[:, 0:1], T.p4i[:, 0:1], -1.0, None, A.mult))

    need("v", k_uof, ldu)
    need("s", k_uof, ldu)
    u1 = did("v", V.tensor_copy(T.urep[:, 0:256], T.u4[:, 0:4].indirect(T.uof[:, 0:16])))
    u2 = did("s", S.activation(T.urep[:, 256:512], T.u4[:, 0:4].indirect(T.uof[:, 16:32]), F.Copy))

    k_gq, k_abs, k_scol, k_k1 = {}, {}, {}, {}

    def codes(a):
        need("v", ld[a])
        c = slice(128 * a, 128 * a + 128)
        k_gq[a] = did("v", V.quantize_mx(T.gq[:, c], T.gs[:, c], T.grt[:, 512 * a:512 * a + 512]))

    def score(a):
        c = slice(128 * a, 128 * a + 128)
        need("t", k_uq, k_gq[a])
        o = slice(512 * a, 512 * a + 128)
        k_row = did("t", TE.matmul_mx(T.psa[:, o], T.uq[:, :], T.us[:, :], T.gq[:, c], T.gs[:, c], True, True))
        k_col = did("t", TE.matmul_mx(T.psb[:, o], T.gq[:, c], T.gs[:, c], T.uq[:, :], T.us[:, :], True, True))
        need("s", k_row)
        k_abs[a] = did("s", S.activation(T.sab[:, c], T.psa[:, o], F.Abs))
        need("s", k_col)
        k_scol[a] = did("s", S.activation(T.scol[:, a:a + 1], T.psb[:, 512 * a:512 * a + 1], F.Abs))
        need("g", k_abs[a])
        k_k1[a] = did("g", g.affine_select(T.k1[:, c], T.sab[:, c], [[-1, 128]], A.is_gt, -1.0, 0, 1))

    codes(0)
    need("v", u1, u2)
    k_uq = did("v", V.quantize_mx(T.uq[:, :], T.us[:, :], T.urep[:, :]))
    for a in (1, 2, 3):
        codes(a)
    for a in range(4):
        score(a)
    k_win = did("v", V.memset(T.win[:, 0:128], 0.0))
    k_p16 = did("v", V.tensor_copy(T.p16f[:, 0:1], T.p16i[:, 0:1]))
    k_tz = did("v", V.tensor_scalar(T.tz[:, 0:1], T.t3[:, 0:1], 1024.0, None, A.add))
    k_dat = did("g", g.iota(T.dat[:, :], [[1, 512]], -255, 0, allow_small_or_imprecise_dtypes=True))

    def against(a, lo, hi):
        at = 640 * a + (lo if lo < 384 else lo + 128)
        need("v", k_scol[a], k_abs[(hi - 1) // 128])
        k, n = None, 128 * a
        if lo < n:
            m = min(n, hi)
            k = did("v", V.tensor_scalar(T.cmp[:, at:at + m - lo], T.sab[:, lo:m], T.scol[:, a:a + 1], None, A.is_ge))
        if n < hi:
            m = max(n, lo)
            k = did("v", V.tensor_scalar(T.cmp[:, at + m - lo:at + hi - lo], T.sab[:, m:hi], T.scol[:, a:a + 1], None, A.is_gt))
        return k

    def ties(a):
        need("v", k_k1[a])
        return did("v", V.tensor_scalar(T.cmp[:, 640 * a + 384:640 * a + 512], T.k1[:, 128 * a:128 * a + 128],
                                        T.scol[:, a:a + 1], None, A.is_equal))

    k_ca = {}

    def first_sum(a, k):
        need("s", k)
        o = slice(640 * a, 640 * a + 384)
        k_ca[a] = did("s", S.activation(T.junk[:, o], T.cmp[:, o], F.Copy, scale=1.0 / 256, accum_out=T.cna[:, a:a + 1]))

    def last_sum(a, k):
        need("s", k, k_ca[a])
        return did("s", S.activation(T.jnk2[:, 256 * a:256 * a + 256], T.cmp[:, 640 * a + 384:640 * a + 640], F.Identity,
                                     bias=T.cna[:, a:a + 1], accum_out=T.cnb[:, a:a + 1]))

    against(0, 0, 256)
    against(1, 0, 256)
    k = against(0, 256, 384)
    first_sum(0, k)
    k = against(1, 256, 384)
    first_sum(1, k)
    k = against(2, 0, 384)
    first_sum(2, k)
    for a in range(3):
        ties(a)
        k = against(a, 384, 512)
        k_cb = last_sum(a, k)
    k1 = against(3, 0, 384)
    ties(3)
    k2 = against(3, 384, 512)
    need("v", k_gi, k_p16)
    k_gd = did("v", V.tensor_scalar(T.gd[:, :], T.gi[:, :], T.p16f[:, 0:1], None, A.add))
    need("v", k1)
    did("v", V.tensor_tensor_scan(T.scn[:, 0:128], T.cmp[:, 1920:2048], T.cmp[:, 2048:2176], 0.0, A.add, A.add))
    need("v", k2)
    did("v", V.tensor_tensor_scan(T.scn[:, 128:256], T.cmp[:, 2176:2304], T.cmp[:, 2304:2432], 0.0, A.add, A.add))
    k3 = did("v", V.tensor_tensor_scan(T.scn[:, 256:320], T.cmp[:, 2432:2496], T.cmp[:, 2496:2560], 0.0, A.add, A.add))
    need("v", k_cb)
    did("v", V.tensor_copy(T.rof[:, 0:3], T.cnb[:, 0:3]))
    need("v", k3)
    k_r = did("v", V.tensor_scalar(T.rof[:, 3:4], T.scn[:, 127:128], T.scn[:, 255:256], T.scn[:, 319:320], A.add, A.add))

    need("v", k_r, k_win, k_gd)
    k_w = did("v", V.tensor_copy(T.win[:, 0:512].indirect(T.rof[:, 0:4]), T.gd[:, :]))
    need("v", k_w)
    did("v", V.tensor_copy(T.win2[:, :, 0:16], T.win[:, 0:128]))
    d2 = did("v", V.tensor_copy(T.win2[:, :, 16:32], T.win[:, 0:128]))
    need("v", d2)
    k_tr = did("v", V.transpose(T.tr[:, :, :], T.win2[:, :, :]))
    need("v", k_tr)
    k_a0 = did("v", V.tensor_tensor(T.a0[:, :], T.tr[:, :, 0], T.tr[:, :, 16], A.add))
    need("v", k_a0)
    k_a1 = did("v", V.tensor_tensor(T.a1[0:64, :], T.a0[0:64, :], T.a0[64:128, :], A.add))
    need("v", k_a1)
    for b in range(4):
        k_a2 = did("v", V.tensor_tensor(T.a2[32 * b:32 * b + 32, :], T.a1[0:32, :], T.a1[32:64, :], A.add))
    lists = [T["lst%d" % s] for s in range(NR)]
    qs = [T["q%d" % s] for s in range(NR)]
    ps = [T["p%d" % s] for s in range(NR)]
    need("v", k_a2)
    k_lst = did("v", V.tensor_scalar(lists[me][:, :], T.a2[:, :], 256.0, None, A.add))
    k_of = {}
    for t in (2, 3, 0, 1):
        k_of[t] = did("v", V.tensor_scalar(T.ofs[:, 8 * t:8 * t + 8], T.a2[:, :], 4.0, 1024.0 + t, A.mult, A.add))
    k_sel = {}
    for t in (0, 1):
        need("v", k_of[t])
        k_sel[t] = did("v", V.tensor_copy(T.sel[:, t:512:4], T.grt[:, 0:2048].indirect(T.ofs[:, 8 * t:8 * t + 8])))
    need("s", k_m4, k_p4)
    k_md = did("s", S.activation(T.m4d[:, :], T.m4[:, :], F.Abs, bias=T.p4n[:, 0:1]))
    did("s", S.activation(T.pw[:, :], T.ones[:, :], F.Copy, scale=-256.0))
    did("s", S.activation(T.rst[:, :], T.ones[:, :], F.Copy))
    need("s", k_md)
    did("s", S.activation(T.mk4[:, :], T.m4d[:, :], F.Relu, bias=1.0, scale=-1.0))
    k_tab = did("s", S.activation(T.tab[:, 0:ZB], T.ones[:, 0:ZB], F.Copy, scale=0.0))
    need("s", k_tab)
    k_rst = did("s", S.activation(T.rst[:, 0:512:4], T.ones[:, 0:128], F.Copy, scale=0.0))
    for t in (2, 3):
        need("s", k_of[t])
        k_sel[t] = did("s", S.activation(T.sel[:, t:512:4], T.grt[:, 0:2048].indirect(T.ofs[:, 8 * t:8 * t + 8]), F.Copy))
    need("v", k_sel[1], k_sel[3])
    k_q = did("v", V.quantize_mx(qs[me][:, :], ps[me][:, :], T.sel[:, :]))

    sent = [0]

    def send(src, dst, sem):
        tr = []
        for c in plan:
            rid, pid, _ = topo.addr(c)
            tr.append(RemoteDMATransfer(dst_ids=[DstId(rid=rid, pnc=pid)], dma_engine_mask=sum(1 << e for e in plan[c]),
                                        remote_sem=T.sem[sem], src=src, dst=dst))
            sent[0] += len(plan[c])
        g.remote_dma_fused(tr, local_sem=T.sem.left)

    need("g", k_lst)
    send(lists[me][:, :], lists[me][:, :], "al%d" % me)
    need("g", k_q)
    send(qs[me][:, :].bitcast(dt.uint8), qs[me][:, :].bitcast(dt.uint8), "ac%d" % me)
    send(ps[me][:, :], ps[me][:, :], "ac%d" % me)

    x, y = late
    order = [0, 1, 2, 3] if x else [1, 0, 2, 3]
    place = {s: i for i, s in enumerate(order)}

    def decode(s, bank, *toks):
        need("t", k_eq[3], *toks)
        r = {}
        for b in range(4):
            r[b] = did("t", TE.matmul_mx(bank[:, 512 * b:512 * b + 128], T.eq[:, 128 * b:128 * b + 128],
                                         T.es[:, 128 * b:128 * b + 128], qs[s][:, :], ps[s][:, :], True, True))
        return r

    def column(s, b):
        o = ZB + 512 * place[s]
        return T.tab[:, o + b:o + 512:4]

    def keep(s, bank, dec):
        r = []
        for b in range(4):
            need("s", dec[b])
            r.append(did("s", S.activation(column(s, b), bank[:, 512 * b:512 * b + 128], F.Copy)))
        return r

    got = {s: ("ac%d" % s, 2 * narr[s]) for s in narr}
    heard = {s: ("al%d" % s, narr[s]) for s in narr}
    heard[me] = k_lst
    k_v = {}

    last = [k_rst]

    def enter(i):
        need("v", heard[order[i]], k_dat, *last)
        last[:] = [did("v", V.tensor_copy(T.pw[:, 0:512].indirect(lists[order[i]][:, 0:8]), T.dat[:, 128 * i:128 * i + 128]))]

    def lookup(i):
        need("v", heard[order[i]], *last)
        last[:] = [did("v", V.tensor_tensor(T.pv[:, 128 * i - 128:128 * i], T.pw[:, 0:512].indirect(lists[order[i]][:, 0:8]),
                                            T.mk4[:, 0:128], A.mult))]
        return last[0]

    def unfold(out, src, n, k):
        need("v", k, k_rst)
        return did("v", V.tensor_tensor_scan(out, T.rst[:, 0:n], src, 0.0, A.mult, A.add))

    def offsets(out, src, k):
        need("v", k, k_tz)
        return did("v", V.tensor_scalar(out, src, 4.0, T.tz[:, 0:1], A.mult, A.add))

    dec = decode(me, T.psa, k_q, k_abs[3])
    need("t", k_scol[3])
    k_sc = did("t", TE.matmul_mx(T.psb[:, 0:128], T.uq[:, :], T.us[:, :], qs[me][:, :], ps[me][:, :], True, True))
    if order[0] == me:
        enter(0)
    k_dif = {}
    for b in range(4):
        need("v", dec[b])
        k_dif[b] = did("v", V.tensor_tensor(T.dif[:, 128 * b:128 * b + 128], T.sel[:, b:512:4],
                                            T.psa[:, 512 * b:512 * b + 128], A.subtract))
    k_ers = [k_er]

    def place_er(h):
        need("v", k_dif[2 * h + 1], *k_ers)
        k_ers[:] = [did("v", V.tensor_copy(T.er32[:, 0:2048].indirect(T.ofs[:, 16 * h:16 * h + 16]),
                                           T.dif[:, 256 * h:256 * h + 256]))]

    place_er(0)
    if order[0] != me:
        enter(0)
    place_er(1)
    kp1 = lookup(1)
    need("y", *k_ers)
    ends = [dma("y", "ster", T.er[:, :], T.er32[:, :])]
    enter(1)
    ku1 = unfold(T.pvs[:, 0:128], T.pv[:, 0:128], 128, kp1)
    lookup(2)
    k_pof1 = offsets(T.pof[:, 0:32], T.pvs[:, 3:128:4], ku1)
    enter(2)
    kp3 = lookup(3)
    enter(3)
    k_places = last[0]
    ku2 = unfold(T.pvs[:, 128:384], T.pv[:, 128:384], 256, kp3)
    k_pof = offsets(T.pof[:, 32:96], T.pvs[:, 131:384:4], ku2)

    k_v[me] = keep(me, T.psa, k_dif)
    need("s", k_sc)
    k_scb = did("s", S.activation(T.scb[:, :], T.psb[:, 0:128], F.Abs))
    need("y", k_scb)
    ends.append(dma("y", "stsc", T.sc[:, :], T.scb[0:1, :]))
    prev = [k_scb]

    def gather_first():
        need("s", k_tab, k_pof1, *k_v[order[0]])
        return did("s", S.activation(T.gsum[:, :], T.tab[:, 0:ZB + 512].indirect(T.pof[:, 0:32]), F.Copy))

    if order[0] == me:
        k_gs = gather_first()
    for s in mates:
        dec = decode(s, T.psb, got[s], *prev)
        k_v[s] = keep(s, T.psb, dec)
        prev = k_v[s]
    if order[0] != me:
        k_gs = gather_first()

    def mask():
        need("s", k_places, k_rst)
        for i in range(4):
            k = did("s", S.activation(T.lw[:, i:512:4], T.pw[:, i:512:4], F.Identity, scale=T.mk4[:, i:i + 1]))
        return k

    dx = decode(x, T.psa, got[x], *k_v[me])
    dy = decode(y, T.psb, got[y], *prev)
    early = order[2] != y
    if early:
        k_lw = mask()
    k_v[y] = keep(y, T.psb, dy)
    if not early:
        k_lw = mask()
    need("v", k_gs)
    total = list(k_v[order[0]])
    for b in range(4):
        need("v", dx[b])
        total.append(did("v", V.tensor_tensor(column(x, b), T.gsum[:, b:512:4], T.psa[:, 512 * b:512 * b + 128], A.add)))
    if early:
        ku = unfold(T.lws[:, :], T.lw[:, :], 512, k_lw)
    for i in (2, 3):
        need("v", k_pof, *k_v[order[i]], *total)
        o = T.tab[:, ZB + 512 * i:ZB + 512 * i + 512]
        total.append(did("v", V.tensor_tensor(o, T.tab[:, 0:ZB + 512 * i].indirect(T.pof[:, 32 * i - 32:32 * i]), o, A.add)))
        if i == 2 and early:
            k_lof = offsets(T.lof[:, :], T.lws[:, 3:512:4], ku)
        if i == 2 and not early:
            ku = unfold(T.lws[:, :], T.lw[:, :], 512, k_lw)
    if not early:
        k_lof = offsets(T.lof[:, :], T.lws[:, 3:512:4], ku)
    k_nb = None
    for s in range(NR):
        need("s", heard[s], k_dat)
        k_nb = did("s", S.activation(T.nbl[:, 128 * s:128 * s + 128], T.dat[:, 0:512].indirect(lists[s][:, 0:8]), F.Copy,
                                     bias=255.0))
    need("y", k_nb)
    ends.append(dma("y", "stnb", T.nb[:, :], T.nbl[0:1, :]))
    need("v", k_lof, k_tab, *total)
    need("s", k_lof, k_tab, *total)
    at = 0
    for i, n in enumerate(PIECES):
        o = T.accs[:, at:at + n]
        window = T.tab[:, 0:TW].indirect(T.lof[:, at // 16:(at + n) // 16])
        if i % 2 == 0:
            k = did("v", V.tensor_copy(o, window))
        else:
            k = did("s", S.activation(o, window, F.Copy))
        need("y", k)
        ends.append(dma("y", "sta%d" % i, T.acc[:, at:at + n], o))
        at += n

    need("y", *ends)
    need("g", ("left", sent[0]), *[(sem, count[sem]) for sem in ("gp", "ve", "se", "te")])
